import numpy as np, ml_dtypes
CORES = [9,25,41,57]
N = 4
BF = ml_dtypes.bfloat16
def gentries(a):
    return np.ascontiguousarray(a.reshape(8, 16, -1).transpose(0, 2, 1)).reshape(8, -1)
def gtable(e):
    e = np.asarray(e); return np.ascontiguousarray(e.reshape(8, -1, 16).transpose(0, 2, 1)).reshape(128, -1).astype(np.int32)
K, C, NS, RO = 256, 4, 896, 6
V, W = C * K, N * C * K
def parts(rng):
    lev = rng.integers(0, 160, (N, 8, 1, W)); b = lev + ((256 - lev) * rng.random((N, 8, 16, W))).astype(np.int64)
    L = rng.integers(0, W, (N, 8, 16, NS)); S = rng.integers(0, W, (N, 8, 16, V))
    P = np.argsort(rng.random((N, 8, C, NS)), axis=-1)[..., :K].reshape(N, 8, V); Q = rng.integers(0, NS, (N, 8, V))
    return np.minimum(b, 255), L, S, P, Q, rng.integers(400, 2000, (N, 8, 16, 1)), rng.integers(1600, 2900, (N, 8, 1))
def pack(b, L, S, P, Q, th, mg):
    return {"base": np.ascontiguousarray(b.reshape(N, 128, W)).astype(np.float32).astype(BF), "favor": np.ascontiguousarray(L.reshape(N, 128, NS)).astype(np.int32),
            "src": np.ascontiguousarray(S.reshape(N, 128, V)).astype(np.int32), "grant": np.stack([gtable(a) for a in P]), "part": np.stack([gtable(a) for a in Q]),
            "th": np.ascontiguousarray(th.reshape(N, 128, 1)).astype(np.int32), "mg": mg.astype(np.int32)}
def setup_inputs(rng):
    return pack(*parts(rng))
def setup_inputs_spread(rng):
    b, L, S, P, Q, th, mg = parts(rng)
    b = np.minimum((256 * rng.random((N, 8, 16, W)) * np.exp2(-rng.integers(0, 8, (N, 8, 1, W)).astype(np.float64))).astype(np.int64), 255)
    L = np.minimum((W * rng.random(L.shape) ** 3).astype(np.int64), W - 1); S = np.minimum((W * rng.random(S.shape) ** 2).astype(np.int64), W - 1)
    Q = np.minimum((NS * rng.random(Q.shape) ** 3).astype(np.int64), NS - 1)
    th = np.minimum(np.exp2(12 * rng.random(th.shape)).astype(np.int64) - 1, 4079); mg = np.minimum(np.exp2(12 * rng.random(mg.shape)).astype(np.int64) - 1, 4079)
    return pack(b, L, S, P, Q, th, mg)
def setup_inputs_ends(rng):
    b, L, S, P, Q, th, mg = parts(rng)
    def tip(x, lo, hi, share):
        m = rng.random(x.shape); return np.where(m < 0.5 * share, lo, np.where(m < share, hi, x))
    sort_ = rng.integers(0, 5, (N, 8, 1, W)); el = 255 * rng.integers(0, 2, b.shape)
    b = np.where(sort_ == 0, 0, np.where(sort_ == 1, 255, np.where(sort_ < 4, el, tip(b, 0, 255, 0.5))))
    L = tip(L, 0, W - 1, 0.7); S = tip(S, 0, W - 1, 0.7); Q = tip(Q, 0, NS - 1, 0.8)
    ix = np.concatenate([np.arange(K // 2), np.arange(NS - K // 2, NS)]); P = rng.permuted(np.tile(ix, (N, 8, C, 1)), axis=-1).reshape(N, 8, V)
    th = tip(th, 0, 4079, 1.0); th[:, :, 15] = 4079; th[:, :, 0] = 0
    for r in range(N):
        last = 4079 if (N - 1 - r) % 2 == 0 else 0
        mg[r, :7, 0] = rng.permutation(np.array([0, 0, 0, 4079, 4079, 4079, 4079 - last])); mg[r, 7, 0] = last
    zero = rng.random((N, 8)) < 0.7; zero[:, 7] = True
    b[..., W - 1] = np.where(zero[:, :, None], 0, b[..., W - 1])
    hi = np.array([0, K + 1, K - 2, 2 * K - 1, V - 1, V - 2 - K]); lo = np.array([K, 1, 2 * K - 2, K - 1, V - 2, V - 1 - K])
    b[:, :, :, hi] = 255; b[:, :, :, lo] = 0; S[:, :, 15, hi] = W - 1; S[:, :, 15, lo] = 0
    np.put_along_axis(L[:, :, 15], P[:, :, hi], W - 1, 2)
    return pack(b, L, S, P, Q, th, mg)
def setup_inputs_corners(rng):
    b, L, S, P, Q, th, mg = parts(rng); e = np.arange(V); rev = (e // K ^ 1) * K + e % K
    for r in range(N):
        for g, k in enumerate(rng.permutation(8)):
            if k == 0: S[r, g] = e
            if k == 1:
                L[r, g] = rng.integers(0, W, (1, NS)); S[r, g] = rng.choice(np.array([0, V - 1, V, W - 1]), (16, V)); Q[r, g] = rng.choice(np.array([0, NS - 1]), V)
            if k == 2:
                b[r, g] = rng.integers(0, 4, (16, W)); th[r, g, :, 0] = rng.integers(0, 41, 16); mg[r, g, 0] = rng.integers(0, 21)
            if k == 3:
                Q[r, g] = P[r, g]; S[r, g] = rev; mg[r, g, 0] = rng.integers(0, 600)
                for c in range(C):
                    a = e[c * K:(c + 1) * K]; L[r, g][:, P[r, g, a]] = np.where(rng.random((16, K)) < 0.5, a, rev[a])
            if k == 4:
                L[r, g] = rng.integers(V, W, (16, NS)); S[r, g] = rng.integers(V, W, (16, V)); th[r, g] = 4079; mg[r, g] = 4079
            if k == 5: th[r, g] = 0; mg[r, g] = 0
            if k == 6:
                b[r, g] = 255 * rng.integers(0, 2, (16, W)); L[r, g, 8:] = L[r, g, :8]; th[r, g, :, 0] = 255 * rng.integers(0, 16, 16); mg[r, g, 0] = 255 * rng.integers(0, 9)
            if k == 7:
                b[r, g] = 8 * rng.integers(0, 32, (1, W)); th[r, g, :, 0] = 128 * rng.integers(1, 20, 16); mg[r, g, 0] = 128 * rng.integers(4, 14)
    return pack(b, L, S, P, Q, th, mg)
def setup_inputs_crowd(rng):
    b, L, S, P, Q, th, mg = parts(rng); z = (1 + (RO - 1) % (N - 1)) * V + ((RO - 1) % C) * K
    s = 490 + np.arange(64); low = (s // 16)[None, :] + (np.arange(16)[:, None] < (s % 16)[None, :]).astype(np.int64)
    for r in range(N):
        for g, k in enumerate(rng.permutation(8) % 4):
            if k == 3: continue
            b[r, g, :, :V] = rng.integers(200, 256, (16, V)); b[r, g, :, z:z + 64] = low; b[r, g, :, z + 64:z + K] = 0
            L[r, g] = z + K - 1 if k == 2 else rng.integers(z + 64, z + K, (16, NS))
            if k == 2: Q[r, g] = rng.integers(0, NS)
            c0 = (1, 0, C - 1)[k]; a = int(rng.integers(0, K)) + K * np.arange(c0, C)
            b[r, g][:, a] = 0; S[r, g][:, a] = z + rng.integers(0, 64, (16, C - c0))
            th[r, g, :, 0] = rng.integers(480, 521, 16); mg[r, g, 0] = rng.choice(np.array([0, 1, 3199]))
    return pack(b, L, S, P, Q, th, mg)
def check_inputs(d):
    bad = []; x = np.asarray(d["base"]).astype(np.float32)
    if not np.all((x >= 0) & (x <= 255) & (x == np.floor(x))): bad.append("range of base")
    for k, lo, hi in (("favor", 0, W - 1), ("src", 0, W - 1), ("grant", 0, NS - 1), ("part", 0, NS - 1), ("th", 0, 4079), ("mg", 0, 4079)):
        if np.min(d[k]) < lo or np.max(d[k]) > hi: bad.append("range of " + k)
    p = np.sort(np.stack([gentries(a) for a in d["grant"]]).astype(np.int64).reshape(N, 8, C, K), axis=-1)
    if np.any(p[..., 1:] == p[..., :-1]): bad.append("grantors of a class differ")
    return bad
def reference(base, favor, src, grant, part, th, mg):
    b = base.astype(np.float32).astype(np.int64).reshape(N, 8, 16, W); X = b + 0
    L = favor.astype(np.int64).reshape(N, 8, 16, NS); S = src.astype(np.int64).reshape(N, 8, 16, V)
    P = np.stack([gentries(a) for a in grant]).astype(np.int64); Q = np.stack([gentries(a) for a in part]).astype(np.int64)
    lim = th.astype(np.int64).reshape(N, 8, 16, 1); gap = mg.astype(np.int64).reshape(N, 8, 1); A = np.zeros((N, 8), np.int64); lane = np.arange(K)
    for t in range(RO):
        c = t % C; o = c * K; v = (c ^ 1) * K; e = o + lane; be = b[..., o:o + K]; old = X[..., o:o + K] + 0; s = S[..., o:o + K] + 0
        far = np.take_along_axis(X, s.reshape(N, 8, 1, 16 * K), 3).reshape(N, 8, 16, 16, K)
        dist = np.sum(np.abs(far - old[:, :, :, None, :]), axis=2)
        lapse = dist > lim + (A & 31)[:, :, None, None]
        x = np.where(lapse, be, old); s = np.where(lapse, e, s)
        pe = P[:, :, None, o:o + K]; T = np.take_along_axis(L, pe, 3)
        y = np.take_along_axis(X, T.reshape(N, 8, 1, 16 * K), 3).reshape(N, 8, 16, 16, K)
        k1 = np.argmin(y, axis=3); least = np.min(y, axis=3); less = least < x
        x = np.where(less, least, x); s = np.where(less, np.take_along_axis(T, k1, 2), s)
        den = np.sum(be - x, axis=2) - np.sum(b[..., v:v + K] - X[..., v:v + K], axis=2) > gap
        k2 = np.sum(y[:, :, :, 0, :], axis=2) & 15
        new = np.take_along_axis(np.take_along_axis(L, Q[:, :, None, o:o + K], 3), k2[:, :, None, :], 2)
        put = den[:, :, None, :] & (np.arange(16)[:, None] == ((lane + t) & 15)[None, :])
        np.put_along_axis(L, np.broadcast_to(pe, T.shape), np.where(put, new, T), 3)
        x = np.where(den[:, :, None, :], be, x); s = np.where(den[:, :, None, :], e, s); A = A + np.sum(den, axis=2)
        d = 1 + t % (N - 1)
        X[..., o:o + K] = x; S[..., o:o + K] = s; X[..., d * V + o:d * V + o + K] = np.roll(x, d, axis=0)
    return {"yx": X.reshape(N, 128, W).astype(np.float32).astype(BF), "ys": S.reshape(N, 128, V).astype(np.float32), "yl": L.reshape(N, 128, NS).astype(np.float32)}

@@ -1,0 +1,429 @@
+from concourse.mybir import AluOpType as A, ActivationFunctionType as AF
+import comms_topo
+
+K, W, V, NS, RO = 256, 4096, 1024, 896, 6
+EARLY = (("S", 0, 80), ("S", 80, 160), ("S", 160, 224), ("S", 224, 256))
+LATE = (("V", 0, 80), ("S", 80, 144), ("S", 144, 192), ("V", 192, 208), ("S", 208, 256))
+EBG = (3, 2, 2, 1, 9)
+LBG = (3, 0, 3, 3, 9, 9)
+CW = 80 * 16
+BF, F3, I3, U1 = "bfloat16", "float32", "int32", "uint16"
+BANKS = ("pB", "pV", "pD", "pK", "pO", "pH", "pJ", "pX")
+_B = {"gr": (64, I3), "pa": (64, I3), "P16": (64, U1), "Q16": (64, U1), "fav": (NS, I3), "Lf": (NS, F3), "Bb": (V, BF),
+      "Si": (V, I3), "S16": (V, U1), "T16": (K, U1), "ysf": (V, F3), "D0": (CW, BF), "RI": (272, BF), "THR": (272, BF),
+      "JR": (512, BF), "JL": (1024, BF), "LE": (512, BF)}
+for _d, _w, _l in ((BF, W, "Xb F0 F1 F2 M0 M1 M2"), (F3, W, "Z Y SCN"), (I3, K, "mi hi h15 s2"),
+                   (F3, K, "Tf Fm0 Fm1 y0a mask mLQ w q s1"),
+                   (BF, K, "mx x1_0 x1_1 sgd0 sgd1 sgl0 sgl1 t0 x04 x05 y0b ones"),
+                   (BF, K, " ".join("xs%d land%d" % (_t, _t) for _t in range(RO))),
+                   (I3, 1, "thc mg8 as0 as1 a63 ki ki2 mgi mq ml"),
+                   (F3, 1, "mgf acc lim0 lim1 lim2 nth kcf mqa mqb mlf ca cb cc ckA ckB"),
+                   (BF, 128, "Ib tb Blk Bp Bn Bneg I5 I14 I22 I12 I256 KC BC MgA MgB"), (BF, 144, "Gm G2 Gn"),
+                   (F3, 128, "If Imf Blkf R8 R8a onf")):
+    for _n in _l.split():
+        _B[_n] = (_w, _d)
+SCRATCH = {n: ("sbuf", [128, w], d) for n, (w, d) in _B.items()}
+for _n in BANKS:
+    SCRATCH[_n] = ("psum", [128, 512], F3)
+SEMAPHORES = ["eV", "eS", "eP", "eG"] + ["d%d" % i for i in range(40)] + ["arr%d" % i for i in range(RO)] + ["loc%d" % i for i in range(RO)]
+
+
+def rank_program(g, core, T, topo):
+    rank = T.rank_of(core)
+    if rank is None:
+        return
+    N = len(T.cores)
+    queue = {"V": g.vector, "S": g.scalar, "P": g.tensor, "G": g, "Y": g.sync}
+    count = {"eV": 0, "eS": 0, "eP": 0, "eG": 0}
+    clk = {q: {} for q in queue}
+    hist = {}
+    ndma = [0]
+
+    def at(name, c0=0, c1=None, step=None, r0=0, r1=128):
+        c1 = (512 if name in BANKS else _B[name][0]) if c1 is None else c1
+        ap = T[name][r0:r1, c0:c1] if step is None else T[name][r0:r1, c0:c1:step]
+        return (ap, name, c0, c1)
+
+    def waits(q, me, ins, outs):
+        cand = {}
+        for wr, regs in ((False, ins), (True, outs)):
+            for (_, name, lo, hi) in regs:
+                for rlo, rhi, rw, rme, rsem, rn, rclk in hist.get(name, ()):
+                    if rme == me and me == "P":
+                        continue
+                    if not (lo < rhi and rlo < hi and (wr or rw)) and (rme == me or name not in BANKS):
+                        continue
+                    if clk[q].get(rsem, 0) < rn and (rsem not in cand or cand[rsem][0] < rn):
+                        cand[rsem] = (rn, rclk)
+        for s in list(cand):
+            n = cand[s][0]
+            if not any(o != s and cand[o][1].get(s, 0) >= n for o in cand):
+                queue[q].wait_ge(T.sem[s], n)
+        for s, (n, rc) in cand.items():
+            for a, b in list(rc.items()) + [(s, n)]:
+                clk[q][a] = max(clk[q].get(a, 0), b)
+
+    def note(q, me, sem, n, ins, outs):
+        count[sem] = n
+        snap = dict(clk[q]) if q else {}
+        snap[sem] = n
+        for w, regs in ((True, outs), (False, ins)):
+            for (_, name, lo, hi) in regs:
+                keep = [r for r in hist.get(name, ()) if not (lo <= r[0] and r[1] <= hi and (w or (r[3] == me and not r[2])))]
+                hist[name] = keep + [(lo, hi, w, me, sem, n, snap)]
+
+    def emit(q, f, outs, ins):
+        if q == "G":
+            outs = outs + [(None, "gq", 0, 1)]
+        waits(q, q, ins, outs)
+        f().then_inc(T.sem["e" + q], 1)
+        note(q, q, "e" + q, count["e" + q] + 1, ins, outs)
+
+    def dma(q, out, in_):
+        outs = [out] if isinstance(out, tuple) else []
+        ins = [in_] if isinstance(in_, tuple) else []
+        s = "d%d" % ndma[0]
+        ndma[0] += 1
+        waits(q, s, ins, outs)
+        queue[q].dma_start(out[0] if outs else out, in_[0] if ins else in_).then_inc(T.sem[s], 16)
+        note(q, s, s, 16, ins, outs)
+
+    def tt(out, a, b, op):
+        emit("V", lambda: g.vector.tensor_tensor(out=out[0], in0=a[0], in1=b[0], op=op), [out], [a, b])
+
+    def ts(out, a, s1, s2, op0, op1=None):
+        ins = [a] + [s for s in (s1, s2) if isinstance(s, tuple)]
+        v1 = s1[0] if isinstance(s1, tuple) else s1
+        v2 = s2[0] if isinstance(s2, tuple) else s2
+        kw = {} if op1 is None else {"op1": op1}
+        emit("V", lambda: g.vector.tensor_scalar(out=out[0], in0=a[0], scalar1=v1, scalar2=v2, op0=op0, **kw), [out], ins)
+
+    def cp(out, a):
+        emit("V", lambda: g.vector.tensor_copy(out=out[0], in_=a[0]), [out], [a])
+
+    def ms(out, c):
+        emit("V", lambda: g.vector.memset(out[0], c), [out], [])
+
+    def act(out, a, func=AF.Identity, bias=0.0, scale=1.0, accum=None):
+        ins = [a] + ([bias] if isinstance(bias, tuple) else [])
+        kw = {} if accum is None else {"accum_out": accum[0]}
+        b = bias[0] if isinstance(bias, tuple) else bias
+        emit("S", lambda: g.scalar.activation(out=out[0], in_=a[0], func=func, bias=b, scale=scale, **kw), [out] + ([accum] if accum else []), ins)
+
+    def mm(out, l, r, start, stop):
+        emit("P", lambda: g.tensor.matmul(out=out[0], lhsT=l[0], rhs=r[0], start=start, stop=stop), [out], [l, r])
+
+    def group(out, pairs):
+        for i, (l, r) in enumerate(pairs):
+            mm(out, l, r, i == 0, i == len(pairs) - 1)
+
+    def gather(q, out, win, off):
+        if q == "S":
+            emit("S", lambda: g.scalar.activation(out=out[0], in_=win[0].indirect(off[0]), func=AF.Copy), [out], [win, off])
+        else:
+            emit("V", lambda: g.vector.tensor_copy(out=out[0], in_=win[0].indirect(off[0])), [out], [win, off])
+
+    dma("Y", at("gr"), T.grant[:])
+    dma("S", at("fav"), T.favor[:])
+    for i in range(4):
+        dma("Y", at("Xb", 1024 * i, 1024 * i + 1024), T.base[:, 1024 * i:1024 * i + 1024])
+    dma("S", at("mg8", r1=8), T.mg[:])
+    dma("S", at("thc"), T.th[:])
+    dma("S", at("pa"), T.part[:])
+    dma("S", at("Si"), T.src[:])
+    dma("Y", at("Bb"), T.base[:, 0:V])
+
+    def iota(out, pattern, base, cm=0, **kw):
+        emit("G", lambda: g.iota(out[0], pattern, base, cm, **kw), [out], [])
+
+    def select(out, a, pattern, op, base, cm):
+        emit("G", lambda: g.affine_select(out[0], a[0], pattern, op, 0.0, base, cm), [out], [a])
+    small = dict(allow_small_or_imprecise_dtypes=True)
+    ms(at("onf", r1=8), 1.0)
+    ms(at("ones"), 1.0)
+    ms(at("JR"), 0.0)
+    select(at("Ib"), at("ones", 0, 128), [[-1, 128]], A.is_equal, 0, 1)
+    iota(at("JR", r0=32, r1=33), [[0, 32], [1, 16]], 0, **small)
+    iota(at("JR", r1=1), [[16, 32], [0, 16]], 0, **small)
+    ms(at("JL", r1=64), 2.0 ** -16)
+    ms(at("JL", r0=64), -128.0)
+    ts(at("JR", r0=32, r1=33), at("JR", r0=32, r1=33), 0.5, None, A.add)
+    ms(at("JR", r0=64, r1=65), 2.0 ** -7)
+    ms(at("JR", r0=96, r1=97), 1.0)
+    iota(at("JL", r0=64, r1=65), [[1, 8], [0, 128]], 120, **small)
+    select(at("tb"), at("ones", 0, 128), [[-16, 8], [0, 16]], A.is_ge, 0, 1)
+    select(at("Blk"), at("tb"), [[16, 8], [0, 16]], A.is_ge, 15, -1)
+    iota(at("ki"), [[0, 1]], 0, 1)
+    select(at("R8a", r1=8), at("onf", r1=8), [[1, 128]], A.is_ge, 0, -16)
+    select(at("R8", r1=8), at("R8a", r1=8), [[-1, 128]], A.is_ge, 15, 16)
+    iota(at("RI"), [[0, 17], [1, 16]], 0, **small)
+    for b in range(8):
+        mm(at(BANKS[b]), at("JL", 128 * b, 128 * b + 128), at("JR"), True, b % 2 == 0)
+    cp(at("P16"), at("gr"))
+    cp(at("Lf"), at("fav"))
+
+    def tgather(t):
+        c = t % 4
+        gather("V", at("T16"), at("Lf"), at("P16", 16 * c, 16 * c + 16))
+    tgather(0)
+    ms(at("D0"), -1.0 / 16)
+    ms(at("D0", 0, CW, 16), 512.0)
+    ms(at("BC", r1=64), 0.0)
+    ms(at("BC", r0=64), 0.0)
+    ms(at("BC", r0=96), -128.0)
+    ts(at("ki2"), at("ki"), 15, None, A.bitwise_and)
+    cp(at("kcf"), at("ki2"))
+    ts(at("THR"), at("RI"), at("kcf"), 2.0 ** 30, A.not_equal, A.mult)
+    cp(at("mgf", r1=8), at("mg8", r1=8))
+    for n, m, v in (("Bp", "Blk", 8192.0), ("Bn", "Blk", -8192.0), ("Blkf", "Blk", 1.0), ("Imf", "Ib", -1.0), ("Bneg", "Blk", -1.0), ("If", "Ib", 65536.0),
+                    ("I5", "Ib", -81920.0), ("I14", "Ib", 16384.0), ("I22", "Ib", -4194304.0), ("I12", "Ib", 4096.0), ("I256", "Ib", 256.0)):
+        act(at(n), at(m), AF.Copy, scale=v)
+    for b in range(8):
+        x = at("Xb", 512 * b, 512 * b + 512)
+        if b % 2 == 0:
+            tt(at("Z", 512 * b, 512 * b + 512), x, at(BANKS[b]), A.add)
+        else:
+            mm(at(BANKS[b]), at("Ib"), x, False, True)
+            act(at("Z", 512 * b, 512 * b + 512), at(BANKS[b]), AF.Copy)
+
+    def consts1():
+        cp(at("Q16"), at("pa"))
+        mm(at("pX", 0, 1), at("R8", r1=8), at("mgf", r1=8), True, True)
+        cp(at("mgi"), at("pX", 0, 1))
+        ts(at("mq"), at("mgi"), 5, None, A.arith_shift_right)
+        ts(at("ml"), at("mgi"), 31, None, A.bitwise_and)
+        ts(at("mqa"), at("mq"), 64.0, -8192.0 * 32, A.add, A.mult)
+        ts(at("mqb"), at("mq"), -8192.0 * 32, None, A.mult)
+        ts(at("mlf"), at("ml"), 0.5, -8192.0, A.add, A.mult)
+        ts(at("ca"), at("kcf"), 0.0, at("mqa"), A.is_equal, A.mult)
+        ts(at("cb"), at("kcf"), 0.0, at("mqb"), A.is_equal, A.mult)
+        ts(at("cc"), at("kcf"), 1.0, at("mlf"), A.is_equal, A.mult)
+        tt(at("ckA"), at("ca"), at("cc"), A.add)
+        tt(at("ckB"), at("cb"), at("cc"), A.add)
+        ts(at("MgA"), at("Blk"), at("ckA"), None, A.mult)
+        ts(at("MgB"), at("Blk"), at("ckB"), None, A.mult)
+
+    def consts2():
+        ms(at("Gm"), 0.0)
+        cp(at("Gm", 15, 128, 16), at("Blk", 0, 128, 16))
+        ts(at("G2"), at("Gm"), 2.0, None, A.mult)
+        ts(at("Gn"), at("Gm"), -1.0, None, A.mult)
+        ms(at("LE", r1=64), 1.0)
+        for c in range(4):
+            ms(at("LE", 128 * c, 128 * c + 128, r0=64), 32768.0 * (16 + c))
+        ms(at("LE", r0=96), -0.5)
+        ms(at("KC", r1=64), 0.0)
+        ms(at("KC", r0=64), -6291456.0 * 128)
+        ms(at("KC", r0=96), -0.5)
+        ts(at("nth"), at("thc"), -1.0, -0.5, A.mult, A.add)
+        cp(at("lim0"), at("nth"))
+        ms(at("as0"), 0)
+        for c in range(1, 4):
+            cp(at("S16", c * K, c * K + K), at("Si", c * K, c * K + K))
+
+    def cls(t):
+        return t % 4, t % 4 * K
+
+    def told(t):
+        return (1 + t % (N - 1)) * V + t % 4 * K
+
+    def bcol(c):
+        return at("Bb", c * K, c * K + K)
+
+    def pre(t):
+        c, o = cls(t)
+        group(at("pB", 0, K), [(at("Ib"), bcol(c)), (at("BC"), at("JR", 0, K))])
+        u = [r for r in range(t) if r % 4 == c ^ 1]
+        mm(at("pV", 0, K), at("Bp"), bcol(c), True, False)
+        mm(at("pV", 0, K), at("MgB" if u else "MgA"), at("ones"), False, False)
+        if u:
+            mm(at("pV", 0, K), at("Bn"), bcol(c ^ 1), False, False)
+            mm(at("pV", 0, K), at("Bp"), at("xs%d" % u[-1]), False, False)
+        if t < RO - 1:
+            for h, n in ((0, o), (K, told(t))):
+                b, s = n // 512, n % 512
+                mm(at("pJ", h, h + K), at("JL", 128 * b, 128 * b + 128, r1=96), at("JR", s, s + K, r1=96), True, True)
+
+    def x0col(t):
+        return at("pB", 0, K) if t < 4 else at("pB", K, 2 * K)
+
+    def fargather(t, h):
+        o, h = t % 4 * K, h * 128
+        gather("S", at("F%d" % (t % 3), 16 * h, 16 * h + 2048), at("Xb"), at("S16", o + h, o + h + 128))
+
+    def farstart(t):
+        c, o = cls(t)
+        old = bcol(c) if t < 4 else at("Xb", o, o + K)
+        for h in (0, 1):
+            mm(at("pO", h, 512, 2), at("Ib"), old, True, True)
+        mm(at("pD", 0, K), at("Bneg"), old, True, False)
+        for p in range(16):
+            mm(at("pD", 0, K), at("Gn", 15 - p, 143 - p), at("F%d" % (t % 3), p, W, 16), False, False)
+
+    def farops(t):
+        f, m = "F%d" % (t % 3), "M%d" % (t % 3)
+
+        def one(p):
+            tt(at(m, 512 * p, 512 * p + 512), at(f, p, W, 8), at("pO"), A.max)
+            for h in (0, 1):
+                mm(at("pD", 0, K), at("G2", 15 - p - 8 * h, 143 - p - 8 * h), at(m, 512 * p + h, 512 * p + 512, 2), False, p == 7 and h == 1)
+        return [lambda p=p: one(p) for p in range(8)]
+
+    def sgnl(t):
+        act(at("sgl%d" % (t % 2)), at("pD", 0, K), AF.Sign, bias=at("lim%d" % (t % 3)))
+
+    def limits(t):
+        a, b = "as%d" % ((t - 1) % 2), "as%d" % (t % 2)
+        tt(at(b), at(a), at("acc"), A.add)
+        ts(at("a63"), at(b), 63, None, A.bitwise_and)
+        ts(at("lim%d" % (t % 3)), at("a63"), -0.5, at("nth"), A.mult, A.add)
+
+    def sgnd(t):
+        act(at("sgd%d" % (t % 2)), at("pV", 0, K), AF.Sign, accum=at("acc"))
+
+    def lapse_x(t):
+        c, o = cls(t)
+        mm(at("pO", 0, K), at("I256"), at("sgl%d" % (t % 2)), True, True)
+        mm(at("pO", K, 2 * K), at("Ib"), bcol(c), True, True)
+        tt(at("t0"), at("Xb", o, o + K), at("pO", 0, K), A.max)
+        tt(at("x0%d" % t), at("t0"), at("pO", K, 2 * K), A.min)
+        group(at("pB", K, 2 * K), [(at("Ib"), at("x0%d" % t)), (at("BC"), at("JR", 0, K))])
+
+    def xbput(n, x):
+        act(at("Xb", n, n + K), at(x), AF.Identity, bias=128.0)
+
+    def schain_pe(t):
+        c, o = cls(t)
+        x0 = bcol(c) if t < 4 else at("x0%d" % t)
+        sd, sl = at("sgd%d" % (t % 2)), at("sgl%d" % (t % 2))
+        group(at("pK", K, 2 * K), [(at("LE", 128 * c, 128 * c + 128), at("JR", 0, K)), (at("I12"), sl), (at("I12"), sd)])
+        group(at("pK", 0, K), [(at("If"), at("Fm%d" % (t % 2))), (at("I5"), at("x1_%d" % (t % 2))), (at("I14"), x0), (at("KC"), at("JR", 0, K)), (at("I22"), sd)])
+
+    def schain_v(t):
+        c, o = cls(t)
+        blk = at("Si", o, o + K)
+        tt(at("s1"), blk, at("pK", K, 2 * K), A.max)
+        tt(at("s2"), at("s1"), at("pK", 0, K), A.max)
+        ts(blk, at("s2"), 4095, None, A.bitwise_and)
+        cp(at("S16" if t < 2 else "ysf", o, o + K), blk)
+        if t >= 2:
+            dma("Y", T.ys[:, o:o + K], at("ysf", o, o + K))
+
+    bg = []
+
+    def run_bg(k):
+        for _ in range(k):
+            if bg:
+                bg.pop(0)()
+
+    for t in range(RO):
+        c, o = cls(t)
+        late = t >= 4
+        if t >= 1:
+            pre(t)
+            limits(t)
+        if late:
+            fargather(t, 0)
+            fargather(t, 1)
+        for ci, (q, a, b) in enumerate(LATE if late else EARLY):
+            y, d0, sc = at("Y", 16 * a, 16 * b), at("D0", 0, 16 * (b - a)), at("SCN", 16 * a, 16 * b)
+            gather(q, y, at("Z"), at("T16", a, b))
+            if t == 0 and ci == 0:
+                consts1()
+                pre(0)
+                cp(at("S16", 0, K), at("Si", 0, K))
+            if not late and ci == 0:
+                run_bg(EBG[0])
+            if late and ci == 1:
+                if t == 4:
+                    farstart(3)
+                    bg.extend(farops(3))
+                    run_bg(99)
+                    sgnl(3)
+                else:
+                    schain_pe(4)
+                    schain_v(4)
+                farstart(t)
+                bg.extend(farops(t))
+                run_bg(LBG[0])
+            if t == 4 and ci == 4:
+                schain_pe(3)
+                schain_v(3)
+            emit("V", lambda: g.vector.tensor_tensor_scan(out=sc[0], data0=d0[0], data1=y[0], initial=512.0, op0=A.add, op1=A.min), [sc], [d0, y])
+            run_bg((LBG if late else EBG)[ci + 1])
+        run_bg(99)
+        if late:
+            sgnl(t)
+            lapse_x(t)
+        act(at("y0a"), at("Y", 0, W, 16), AF.Identity, bias=12582912.0)
+        act(at("y0b"), at("y0a"), AF.Identity, bias=-12582912.0)
+        gather("S", at("Tf"), at("Lf"), at("P16", 16 * c, 16 * c + 16))
+        x1, xs, R = at("x1_%d" % (t % 2)), at("xs%d" % t), at("SCN", 15, W, 16)
+        ts(at("mi"), R, -0.5, None, A.add)
+        tt(x1, at("mi"), x0col(t), A.min)
+        mm(at("pV", 0, K), at("Bn"), x1, False, True)
+        mm(at("pH", 0, K), at("Blk"), at("y0b"), True, True)
+        tt(at("mx"), x1, at("pV", 0, K), A.max)
+        tt(xs, at("mx"), at("pB", 0, K), A.min)
+        d = 1 + t % (N - 1)
+        nxt, prv = T.cores[(rank + d) % N], T.cores[(rank - d) % N]
+        arr, loc = "arr%d" % t, "loc%d" % t
+        waits("G", loc, [xs], [])
+        rid, pid, _ = topo.addr(nxt)
+        g.remote_dma(out_ap=T["land%d" % t][:], in_ap=xs[0], remote_sem=T.sem[arr], local_sem=T.sem[loc],
+                     pid=pid, routing_id=rid, dma_engine_mask=topo.mask(core, nxt))
+        note("G", loc, loc, len(topo.engines(core, nxt)), [xs], [])
+        note(None, arr, arr, len(topo.engines(prv, core)), [], [at("land%d" % t)])
+        if not late:
+            if t > 0:
+                xbput(o - K, "xs%d" % (t - 1))
+                xbput(told(t - 1), "land%d" % (t - 1))
+            fargather(t, 0)
+            if t > 0:
+                sgnl(t - 1)
+                schain_pe(t - 1)
+            sgnd(t)
+            fargather(t, 1)
+        else:
+            sgnd(t)
+        if t >= 3:
+            xbput(o, "xs%d" % t)
+            if t < RO - 1:
+                xbput(told(t), "land%d" % t)
+        if t < RO - 1:
+            tt(at("Z", o, o + K), xs, at("pJ", 0, K), A.add)
+        cp(at("hi"), at("pH", 0, K))
+        ts(at("h15"), at("hi"), 15, None, A.bitwise_and)
+        ts(at("mask"), at("h15"), at("kcf"), None, A.is_equal)
+        qo, po = at("Q16", 16 * c, 16 * c + 16), at("P16", 16 * c, 16 * c + 16)
+        emit("V", lambda: g.vector.tensor_tensor(out=T.mLQ[:], in0=T.Lf[:].indirect(qo[0]), in1=T.mask[:], op=A.mult), [at("mLQ")], [at("Lf"), qo, at("mask")])
+        group(at("pH", K, 2 * K), [(at("Imf"), at("Tf")), (at("Blkf"), at("mLQ"))])
+        tt(at("w"), at("pV", 0, K), at("THR", t, t + K), A.is_gt)
+        tt(at("Fm%d" % (t % 2)), R, x0col(t), A.min)
+        if t == 0:
+            consts2()
+        if 0 < t < 4:
+            schain_v(t - 1)
+        tt(at("q"), at("pH", K, 2 * K), at("w"), A.mult)
+        emit("V", lambda: g.vector.tensor_tensor(out=T.Lf[:].indirect(po[0]), in0=T.q[:], in1=T.Tf[:], op=A.add), [at("Lf")], [at("q"), at("Tf"), po])
+        if t < RO - 1:
+            tgather(t + 1)
+            n = told(t)
+            tt(at("Z", n, n + K), at("land%d" % t), at("pJ", K, 2 * K), A.add)
+        if t < 3:
+            farstart(t)
+            bg.extend(farops(t))
+        if t == 2:
+            for lo, hi in ((1280, 1792), (2560, 3328), (3840, 4096)):
+                dma("Y", T.yx[:, lo:hi], at("Xb", lo, hi))
+    dma("Y", T.yl[:], at("Lf"))
+    for lo, hi in ((0, 1280), (1792, 2560), (3584, 3840)):
+        dma("Y", T.yx[:, lo:hi], at("Xb", lo, hi))
+    schain_pe(RO - 1)
+    n = told(RO - 1)
+    xbput(n, "land%d" % (RO - 1))
+    dma("Y", T.yx[:, n:n + K], at("Xb", n, n + K))
+    schain_v(RO - 1)
+    for s, n in count.items():
+        if n and clk["Y"].get(s, 0) < n:
+            g.sync.wait_ge(T.sem[s], n)

@@ -2,30 +2,73 @@ from concourse.mybir import AluOpType as A, ActivationFunctionType as AF
 import comms_topo
 
 K, W, V, NS, RO = 256, 4096, 1024, 896, 6
-EARLY = (("S", 0, 80), ("S", 80, 160), ("S", 160, 224), ("S", 224, 256))
-LATE = (("V", 0, 80), ("S", 80, 144), ("S", 144, 192), ("V", 192, 208), ("S", 208, 256))
-EBG = (3, 2, 2, 1, 9)
-LBG = (3, 0, 3, 3, 9, 9)
-CW = 80 * 16
-BF, F3, I3, U1 = "bfloat16", "float32", "int32", "uint16"
-BANKS = ("pB", "pV", "pD", "pK", "pO", "pH", "pJ", "pX")
-_B = {"gr": (64, I3), "pa": (64, I3), "P16": (64, U1), "Q16": (64, U1), "fav": (NS, I3), "Lf": (NS, F3), "Bb": (V, BF),
-      "Si": (V, I3), "S16": (V, U1), "T16": (K, U1), "ysf": (V, F3), "D0": (CW, BF), "RI": (272, BF), "THR": (272, BF),
-      "JR": (512, BF), "JL": (1024, BF), "LE": (512, BF)}
-for _d, _w, _l in ((BF, W, "Xb F0 F1 F2 M0 M1 M2"), (F3, W, "Z Y SCN"), (I3, K, "mi hi h15 s2"),
-                   (F3, K, "Tf Fm0 Fm1 y0a mask mLQ w q s1"),
-                   (BF, K, "mx x1_0 x1_1 sgd0 sgd1 sgl0 sgl1 t0 x04 x05 y0b ones"),
-                   (BF, K, " ".join("xs%d land%d" % (_t, _t) for _t in range(RO))),
-                   (I3, 1, "thc mg8 as0 as1 a63 ki ki2 mgi mq ml"),
-                   (F3, 1, "mgf acc lim0 lim1 lim2 nth kcf mqa mqb mlf ca cb cc ckA ckB"),
-                   (BF, 128, "Ib tb Blk Bp Bn Bneg I5 I14 I22 I12 I256 KC BC MgA MgB"), (BF, 144, "Gm G2 Gn"),
-                   (F3, 128, "If Imf Blkf R8 R8a onf")):
+MAGIC = 12582912.0
+KEYS = ((0, 24), (24, 64), (64, 120), (120, 192), (192, 256))
+PARTS = ((0, 256),)
+PIECE = 32
+LATE = (("F", 0, 64), ("k", 0, 24), ("k", 24, 64), ("k", 64, 120), ("K", 0, 24), ("K", 24, 64), ("f", 64, 128), ("K", 64, 120),
+        ("k", 120, 192), ("M", 0, 128), ("f", 128, 256), ("K", 120, 192), ("k", 192, 256), ("M", 128, 256), ("K", 192, 256))
+GATHER, SCATTER, PE, WAKE, DMA, HOP = 1.56, 3.8, 0.75, 80, 2000, 4300
+BF, HF, F3, I3, U1 = "bfloat16", "float16", "float32", "int32", "uint16"
+BANKS = ("pB", "pW", "pD", "pK", "pT", "pH", "pJ", "pO")
+_B = {"gr": (64, I3), "pa": (64, I3), "P16": (64, U1), "Q16": (64, U1), "fav": (NS, I3), "Lf": (NS, F3),
+      "Si": (V, I3), "S16": (V, U1), "T16": (K, U1), "ysf": (V, F3), "D0": (W // 2, BF), "RI": (272, BF), "NP": (272, BF),
+      "JR": (512, BF), "JL": (1024, BF), "LE": (512, BF), "CM": (512, BF), "acc": (RO * len(PARTS), F3)}
+for _d, _w, _l in ((BF, W, "X0 X1 X2 X3 X4 X5 F0 F1 F2 F3 M0 M1 M2"), (F3, W, "Z"), (F3, W // 2, "YS YV SCN"), (I3, K, "hi z s2"),
+                   (F3, K, "Tf mLQ q s1 ok y0a " + " ".join("Fm%d" % _t for _t in range(RO))), (HF, K, "Th"),
+                   (BF, K, "x04 x05 ones bT xs5 land5 y0b"),
+                   (BF, K, " ".join("x1_%d w%d nl%d" % (_t, _t, _t) for _t in range(RO))),
+                   (I3, 1, "thc mg8 as0 as1 a31 ki ki2 thi tlo"),
+                   (F3, 1, "mgf mgb kcf ck nhi lim lim0"),
+                   (BF, 128, "Ib Im ta tb Blk Bneg B2 B8 B12 B13 B24 I17 I16 I13 I8 Dhi"), (BF, 128 * RO, "Dlo"),
+                   (BF, 144, "WA WB"), (F3, 128, "If Blkf R8 R8a onf")):
     for _n in _l.split():
         _B[_n] = (_w, _d)
 SCRATCH = {n: ("sbuf", [128, w], d) for n, (w, d) in _B.items()}
 for _n in BANKS:
-    SCRATCH[_n] = ("psum", [128, 512], F3)
-SEMAPHORES = ["eV", "eS", "eP", "eG"] + ["d%d" % i for i in range(40)] + ["arr%d" % i for i in range(RO)] + ["loc%d" % i for i in range(RO)]
+    _B[_n] = (1024, BF) if _n == "pO" else (512, F3)
+    SCRATCH[_n] = ("psum", [128, _B[_n][0]], _B[_n][1])
+SEMAPHORES = ["eV", "eS", "eP", "eG"] + ["d%d" % i for i in range(60)] + [n + "%d_%d" % (t, a) for n in ("arr", "loc") for t in range(RO) for a, _ in PARTS]
+
+
+def in_order(calls):
+    seen, after, row = {}, [], {}
+    for i, (q, _, outs, ins, _, _, line) in enumerate(calls):
+        dep = set()
+        for wr, regs in ((False, ins), (True, outs)):
+            for r in regs:
+                for j, a, b, w in seen.get(r[1], ()):
+                    if (wr or w) and (r[2] < b and a < r[3] or calls[j][0] == q == "P" and r[1] in BANKS):
+                        dep.add(j)
+        for wr, regs in ((True, outs), (False, ins)):
+            for r in regs:
+                keep = [e for e in seen.get(r[1], ()) if not (wr and r[2] <= e[1] and e[2] <= r[3] and (q == "P" or r[1] not in BANKS))]
+                seen[r[1]] = keep + [(i, r[2], r[3], wr)]
+        after.append({j: calls[j][4] + calls[j][5] + (0 if calls[j][0] == q == "P" else WAKE) for j in dep - {i}})
+        if line in row:
+            after[i].setdefault(row[line], calls[row[line]][4])
+        if line:
+            row[line] = i
+    way = [c[4] + c[5] for c in calls]
+    for i in reversed(range(len(calls))):
+        for j in after[i]:
+            way[j] = max(way[j], after[i][j] + way[i])
+    start, busy = {}, {}
+    for i in sorted(range(len(calls)), key=lambda i: (-way[i], i)):
+        q, _, outs, ins, cost, more, _ = calls[i]
+        need = [(q, cost)] + [(b, cost) for b in sorted({r[1] for r in outs + ins if r[1] in BANKS})] + ([("dma", more - DMA)] if more else [])
+        t = max([start[j] + after[i][j] for j in after[i]], default=0)
+        moved = True
+        while moved:
+            moved = False
+            for res, d in need:
+                for a, b in busy.get(res, ()):
+                    if a < t + d and t < b:
+                        t, moved = b, True
+        start[i] = t
+        for res, d in need:
+            busy[res] = sorted(busy.get(res, []) + [(t, t + d)])
+    return sorted(start, key=lambda i: (start[i], i))
 
 
 def rank_program(g, core, T, topo):
@@ -37,17 +80,17 @@ def rank_program(g, core, T, topo):
     count = {"eV": 0, "eS": 0, "eP": 0, "eG": 0}
     clk = {q: {} for q in queue}
     hist = {}
-    ndma = [0]
+    calls = []
 
-    def at(name, c0=0, c1=None, step=None, r0=0, r1=128):
-        c1 = (512 if name in BANKS else _B[name][0]) if c1 is None else c1
-        ap = T[name][r0:r1, c0:c1] if step is None else T[name][r0:r1, c0:c1:step]
-        return (ap, name, c0, c1)
+    def at(name, c0=0, c1=None, step=1, r0=0, r1=128):
+        c1 = _B[name][0] if c1 is None else c1
+        ap = T[name][r0:r1, c0:c1] if step == 1 else T[name][r0:r1, c0:c1:step]
+        return (ap, name, c0, c1, -(-(c1 - c0) // step))
 
     def waits(q, me, ins, outs):
         cand = {}
         for wr, regs in ((False, ins), (True, outs)):
-            for (_, name, lo, hi) in regs:
+            for (_, name, lo, hi, _) in regs:
                 for rlo, rhi, rw, rme, rsem, rn, rclk in hist.get(name, ()):
                     if rme == me and me == "P":
                         continue
@@ -68,158 +111,92 @@ def rank_program(g, core, T, topo):
         snap = dict(clk[q]) if q else {}
         snap[sem] = n
         for w, regs in ((True, outs), (False, ins)):
-            for (_, name, lo, hi) in regs:
+            for (_, name, lo, hi, _) in regs:
                 keep = [r for r in hist.get(name, ()) if not (lo <= r[0] and r[1] <= hi and (w or (r[3] == me and not r[2])))]
                 hist[name] = keep + [(lo, hi, w, me, sem, n, snap)]
 
-    def emit(q, f, outs, ins):
-        if q == "G":
-            outs = outs + [(None, "gq", 0, 1)]
-        waits(q, q, ins, outs)
-        f().then_inc(T.sem["e" + q], 1)
-        note(q, q, "e" + q, count["e" + q] + 1, ins, outs)
+    def emit(q, f, outs, ins, cost, line=None):
+        def issue():
+            o = outs + [(None, "gq", 0, 1, 1)] if q == "G" else outs
+            waits(q, q, ins, o)
+            f().then_inc(T.sem["e" + q], 1)
+            note(q, q, "e" + q, count["e" + q] + 1, ins, o)
+        calls.append((q, issue, outs, ins, max(32 if q == "P" else 64, cost), 0, line))
 
-    def dma(q, out, in_):
+    def dma(out, in_, size, line=None):
         outs = [out] if isinstance(out, tuple) else []
         ins = [in_] if isinstance(in_, tuple) else []
-        s = "d%d" % ndma[0]
-        ndma[0] += 1
-        waits(q, s, ins, outs)
-        queue[q].dma_start(out[0] if outs else out, in_[0] if ins else in_).then_inc(T.sem[s], 16)
-        note(q, s, s, 16, ins, outs)
+        s = "d%d" % sum(c[0] == "Y" for c in calls)
 
-    def tt(out, a, b, op):
-        emit("V", lambda: g.vector.tensor_tensor(out=out[0], in0=a[0], in1=b[0], op=op), [out], [a, b])
+        def issue():
+            waits("Y", s, ins, outs)
+            g.sync.dma_start(out[0] if outs else out, in_[0] if ins else in_).then_inc(T.sem[s], 16)
+            note("Y", s, s, 16, ins, outs)
+        calls.append(("Y", issue, outs, ins, 64, DMA + 500 + size // 2, line))
+
+    def half(*regs):
+        return 0.5 if all(_B[r[1]][1] in (BF, HF, U1) for r in regs) else 1
+
+    def tt(out, a, b, op, line=None):
+        rate = half(out, a, b) * (1 if a[1] in BANKS or b[1] in BANKS else 2)
+        emit("V", lambda: g.vector.tensor_tensor(out=out[0], in0=a[0], in1=b[0], op=op), [out], [a, b], out[4] * rate, line)
 
     def ts(out, a, s1, s2, op0, op1=None):
         ins = [a] + [s for s in (s1, s2) if isinstance(s, tuple)]
         v1 = s1[0] if isinstance(s1, tuple) else s1
         v2 = s2[0] if isinstance(s2, tuple) else s2
         kw = {} if op1 is None else {"op1": op1}
-        emit("V", lambda: g.vector.tensor_scalar(out=out[0], in0=a[0], scalar1=v1, scalar2=v2, op0=op0, **kw), [out], ins)
+        emit("V", lambda: g.vector.tensor_scalar(out=out[0], in0=a[0], scalar1=v1, scalar2=v2, op0=op0, **kw), [out], ins, out[4] * half(out, a))
 
     def cp(out, a):
-        emit("V", lambda: g.vector.tensor_copy(out=out[0], in_=a[0]), [out], [a])
+        emit("V", lambda: g.vector.tensor_copy(out=out[0], in_=a[0]), [out], [a], out[4] * half(out, a))
 
     def ms(out, c):
-        emit("V", lambda: g.vector.memset(out[0], c), [out], [])
+        emit("V", lambda: g.vector.memset(out[0], c), [out], [], out[4] * half(out))
 
-    def act(out, a, func=AF.Identity, bias=0.0, scale=1.0, accum=None):
-        ins = [a] + ([bias] if isinstance(bias, tuple) else [])
+    def act(out, a, func=AF.Copy, bias=0.0, scale=1.0, accum=None, off=None, line=None):
+        ins = [a] + ([bias] if isinstance(bias, tuple) else []) + ([off] if off else [])
         kw = {} if accum is None else {"accum_out": accum[0]}
         b = bias[0] if isinstance(bias, tuple) else bias
-        emit("S", lambda: g.scalar.activation(out=out[0], in_=a[0], func=func, bias=b, scale=scale, **kw), [out] + ([accum] if accum else []), ins)
+        src = a[0].indirect(off[0]) if off else a[0]
+        emit("S", lambda: g.scalar.activation(out=out[0], in_=src, func=func, bias=b, scale=scale, **kw), [out] + ([accum] if accum else []), ins,
+             80 + out[4] * GATHER if off else out[4], line)
 
     def mm(out, l, r, start, stop):
-        emit("P", lambda: g.tensor.matmul(out=out[0], lhsT=l[0], rhs=r[0], start=start, stop=stop), [out], [l, r])
+        emit("P", lambda: g.tensor.matmul(out=out[0], lhsT=l[0], rhs=r[0], start=start, stop=stop), [out], [l, r], PE * max(64, r[4]) * (1 if half(r) < 1 else 4))
 
-    def group(out, pairs):
+    def group(out, pairs, start=True, stop=True):
         for i, (l, r) in enumerate(pairs):
-            mm(out, l, r, i == 0, i == len(pairs) - 1)
+            mm(out, l, r, start and i == 0, stop and i == len(pairs) - 1)
 
-    def gather(q, out, win, off):
-        if q == "S":
-            emit("S", lambda: g.scalar.activation(out=out[0], in_=win[0].indirect(off[0]), func=AF.Copy), [out], [win, off])
+    def turn(out, a):
+        emit("P", lambda: g.tensor.transpose(out[0], a[0], T.Ib[:]), [out], [a, at("Ib")], 128 * PE)
+
+    def vgather(out, win, off, b=None, op=None, line=None):
+        if b is None:
+            emit("V", lambda: g.vector.tensor_copy(out=out[0], in_=win[0].indirect(off[0])), [out], [win, off], 60 + out[4] * GATHER, line)
         else:
-            emit("V", lambda: g.vector.tensor_copy(out=out[0], in_=win[0].indirect(off[0])), [out], [win, off])
-
-    dma("Y", at("gr"), T.grant[:])
-    dma("S", at("fav"), T.favor[:])
-    for i in range(4):
-        dma("Y", at("Xb", 1024 * i, 1024 * i + 1024), T.base[:, 1024 * i:1024 * i + 1024])
-    dma("S", at("mg8", r1=8), T.mg[:])
-    dma("S", at("thc"), T.th[:])
-    dma("S", at("pa"), T.part[:])
-    dma("S", at("Si"), T.src[:])
-    dma("Y", at("Bb"), T.base[:, 0:V])
+            emit("V", lambda: g.vector.tensor_tensor(out=out[0], in0=win[0].indirect(off[0]), in1=b[0], op=op), [out], [win, off, b], 60 + out[4] * GATHER, line)
 
     def iota(out, pattern, base, cm=0, **kw):
-        emit("G", lambda: g.iota(out[0], pattern, base, cm, **kw), [out], [])
+        emit("G", lambda: g.iota(out[0], pattern, base, cm, **kw), [out], [], 160 + 2 * out[4])
 
     def select(out, a, pattern, op, base, cm):
-        emit("G", lambda: g.affine_select(out[0], a[0], pattern, op, 0.0, base, cm), [out], [a])
-    small = dict(allow_small_or_imprecise_dtypes=True)
-    ms(at("onf", r1=8), 1.0)
-    ms(at("ones"), 1.0)
-    ms(at("JR"), 0.0)
-    select(at("Ib"), at("ones", 0, 128), [[-1, 128]], A.is_equal, 0, 1)
-    iota(at("JR", r0=32, r1=33), [[0, 32], [1, 16]], 0, **small)
-    iota(at("JR", r1=1), [[16, 32], [0, 16]], 0, **small)
-    ms(at("JL", r1=64), 2.0 ** -16)
-    ms(at("JL", r0=64), -128.0)
-    ts(at("JR", r0=32, r1=33), at("JR", r0=32, r1=33), 0.5, None, A.add)
-    ms(at("JR", r0=64, r1=65), 2.0 ** -7)
-    ms(at("JR", r0=96, r1=97), 1.0)
-    iota(at("JL", r0=64, r1=65), [[1, 8], [0, 128]], 120, **small)
-    select(at("tb"), at("ones", 0, 128), [[-16, 8], [0, 16]], A.is_ge, 0, 1)
-    select(at("Blk"), at("tb"), [[16, 8], [0, 16]], A.is_ge, 15, -1)
-    iota(at("ki"), [[0, 1]], 0, 1)
-    select(at("R8a", r1=8), at("onf", r1=8), [[1, 128]], A.is_ge, 0, -16)
-    select(at("R8", r1=8), at("R8a", r1=8), [[-1, 128]], A.is_ge, 15, 16)
-    iota(at("RI"), [[0, 17], [1, 16]], 0, **small)
-    for b in range(8):
-        mm(at(BANKS[b]), at("JL", 128 * b, 128 * b + 128), at("JR"), True, b % 2 == 0)
-    cp(at("P16"), at("gr"))
-    cp(at("Lf"), at("fav"))
+        emit("G", lambda: g.affine_select(out[0], a[0], pattern, op, 0.0, base, cm), [out], [a], 200 + 2 * out[4])
 
-    def tgather(t):
-        c = t % 4
-        gather("V", at("T16"), at("Lf"), at("P16", 16 * c, 16 * c + 16))
-    tgather(0)
-    ms(at("D0"), -1.0 / 16)
-    ms(at("D0", 0, CW, 16), 512.0)
-    ms(at("BC", r1=64), 0.0)
-    ms(at("BC", r0=64), 0.0)
-    ms(at("BC", r0=96), -128.0)
-    ts(at("ki2"), at("ki"), 15, None, A.bitwise_and)
-    cp(at("kcf"), at("ki2"))
-    ts(at("THR"), at("RI"), at("kcf"), 2.0 ** 30, A.not_equal, A.mult)
-    cp(at("mgf", r1=8), at("mg8", r1=8))
-    for n, m, v in (("Bp", "Blk", 8192.0), ("Bn", "Blk", -8192.0), ("Blkf", "Blk", 1.0), ("Imf", "Ib", -1.0), ("Bneg", "Blk", -1.0), ("If", "Ib", 65536.0),
-                    ("I5", "Ib", -81920.0), ("I14", "Ib", 16384.0), ("I22", "Ib", -4194304.0), ("I12", "Ib", 4096.0), ("I256", "Ib", 256.0)):
-        act(at(n), at(m), AF.Copy, scale=v)
-    for b in range(8):
-        x = at("Xb", 512 * b, 512 * b + 512)
-        if b % 2 == 0:
-            tt(at("Z", 512 * b, 512 * b + 512), x, at(BANKS[b]), A.add)
-        else:
-            mm(at(BANKS[b]), at("Ib"), x, False, True)
-            act(at("Z", 512 * b, 512 * b + 512), at(BANKS[b]), AF.Copy)
+    def tell(t, a, b):
+        d = 1 + t % (N - 1)
+        nxt, prv = T.cores[(rank + d) % N], T.cores[(rank - d) % N]
+        arr, loc, xs, land = "arr%d_%d" % (t, a), "loc%d_%d" % (t, a), xs_of(t, a, b), land_of(t, a, b)
 
-    def consts1():
-        cp(at("Q16"), at("pa"))
-        mm(at("pX", 0, 1), at("R8", r1=8), at("mgf", r1=8), True, True)
-        cp(at("mgi"), at("pX", 0, 1))
-        ts(at("mq"), at("mgi"), 5, None, A.arith_shift_right)
-        ts(at("ml"), at("mgi"), 31, None, A.bitwise_and)
-        ts(at("mqa"), at("mq"), 64.0, -8192.0 * 32, A.add, A.mult)
-        ts(at("mqb"), at("mq"), -8192.0 * 32, None, A.mult)
-        ts(at("mlf"), at("ml"), 0.5, -8192.0, A.add, A.mult)
-        ts(at("ca"), at("kcf"), 0.0, at("mqa"), A.is_equal, A.mult)
-        ts(at("cb"), at("kcf"), 0.0, at("mqb"), A.is_equal, A.mult)
-        ts(at("cc"), at("kcf"), 1.0, at("mlf"), A.is_equal, A.mult)
-        tt(at("ckA"), at("ca"), at("cc"), A.add)
-        tt(at("ckB"), at("cb"), at("cc"), A.add)
-        ts(at("MgA"), at("Blk"), at("ckA"), None, A.mult)
-        ts(at("MgB"), at("Blk"), at("ckB"), None, A.mult)
-
-    def consts2():
-        ms(at("Gm"), 0.0)
-        cp(at("Gm", 15, 128, 16), at("Blk", 0, 128, 16))
-        ts(at("G2"), at("Gm"), 2.0, None, A.mult)
-        ts(at("Gn"), at("Gm"), -1.0, None, A.mult)
-        ms(at("LE", r1=64), 1.0)
-        for c in range(4):
-            ms(at("LE", 128 * c, 128 * c + 128, r0=64), 32768.0 * (16 + c))
-        ms(at("LE", r0=96), -0.5)
-        ms(at("KC", r1=64), 0.0)
-        ms(at("KC", r0=64), -6291456.0 * 128)
-        ms(at("KC", r0=96), -0.5)
-        ts(at("nth"), at("thc"), -1.0, -0.5, A.mult, A.add)
-        cp(at("lim0"), at("nth"))
-        ms(at("as0"), 0)
-        for c in range(1, 4):
-            cp(at("S16", c * K, c * K + K), at("Si", c * K, c * K + K))
+        def issue():
+            waits("G", loc, [xs], [])
+            rid, pid, _ = topo.addr(nxt)
+            g.remote_dma(out_ap=land[0], in_ap=xs[0], remote_sem=T.sem[arr], local_sem=T.sem[loc],
+                         pid=pid, routing_id=rid, dma_engine_mask=topo.mask(core, nxt))
+            note("G", loc, loc, len(topo.engines(core, nxt)), [xs], [])
+            note(None, arr, arr, len(topo.engines(prv, core)), [], [land])
+        calls.append(("G", issue, [land], [xs], 600, HOP - 4 * (K - b + a), None))
 
     def cls(t):
         return t % 4, t % 4 * K
@@ -227,203 +204,239 @@ def rank_program(g, core, T, topo):
     def told(t):
         return (1 + t % (N - 1)) * V + t % 4 * K
 
-    def bcol(c):
-        return at("Bb", c * K, c * K + K)
+    def bcol(c, a=0, b=K):
+        return at("X0", c * K + a, c * K + b)
 
-    def pre(t):
-        c, o = cls(t)
-        group(at("pB", 0, K), [(at("Ib"), bcol(c)), (at("BC"), at("JR", 0, K))])
-        u = [r for r in range(t) if r % 4 == c ^ 1]
-        mm(at("pV", 0, K), at("Bp"), bcol(c), True, False)
-        mm(at("pV", 0, K), at("MgB" if u else "MgA"), at("ones"), False, False)
-        if u:
-            mm(at("pV", 0, K), at("Bn"), bcol(c ^ 1), False, False)
-            mm(at("pV", 0, K), at("Bp"), at("xs%d" % u[-1]), False, False)
-        if t < RO - 1:
-            for h, n in ((0, o), (K, told(t))):
-                b, s = n // 512, n % 512
-                mm(at("pJ", h, h + K), at("JL", 128 * b, 128 * b + 128, r1=96), at("JR", s, s + K, r1=96), True, True)
+    def xs_of(t, a=0, b=K):
+        return at("X%d" % (t + 1), t % 4 * K + a, t % 4 * K + b) if t < RO - 1 else at("xs5", a, b)
 
-    def x0col(t):
-        return at("pB", 0, K) if t < 4 else at("pB", K, 2 * K)
+    def land_of(t, a=0, b=K):
+        return at("X%d" % (t + 1), told(t) + a, told(t) + b) if t < RO - 1 else at("land5", a, b)
 
-    def fargather(t, h):
-        o, h = t % 4 * K, h * 128
-        gather("S", at("F%d" % (t % 3), 16 * h, 16 * h + 2048), at("Xb"), at("S16", o + h, o + h + 128))
+    def const(i):
+        return (at("CM", 128 * i, 128 * i + 128, r0=64), at("JR", 0, K, r0=64))
 
-    def farstart(t):
-        c, o = cls(t)
-        old = bcol(c) if t < 4 else at("Xb", o, o + K)
-        for h in (0, 1):
-            mm(at("pO", h, 512, 2), at("Ib"), old, True, True)
-        mm(at("pD", 0, K), at("Bneg"), old, True, False)
-        for p in range(16):
-            mm(at("pD", 0, K), at("Gn", 15 - p, 143 - p), at("F%d" % (t % 3), p, W, 16), False, False)
+    def carry(t):
+        o, n = t % 4 * K, told(t)
+        for lo, hi in ((0, o), (o + K, n), (n + K, W)):
+            if lo < hi:
+                dma(at("X%d" % (t + 1), lo, hi) if t < RO - 1 else T.yx[:, lo:hi], at("X%d" % t, lo, hi), 2 * (hi - lo), "loads")
 
-    def farops(t):
-        f, m = "F%d" % (t % 3), "M%d" % (t % 3)
+    loads = [(at("gr"), T.grant[:]), (at("fav"), T.favor[:])] + [(at("X0", V * i, V * i + V), T.base[:, V * i:V * i + V]) for i in range(N)]
+    loads += [(at("Si", 0, K), T.src[:, 0:K]), (at("pa"), T.part[:]), (at("mg8", r1=8), T.mg[:]), (at("thc"), T.th[:]), (at("Si", K, V), T.src[:, K:V])]
+    for to, of in loads:
+        dma(to, of, int(to[4] * 4 * half(to)), "loads")
 
-        def one(p):
-            tt(at(m, 512 * p, 512 * p + 512), at(f, p, W, 8), at("pO"), A.max)
-            for h in (0, 1):
-                mm(at("pD", 0, K), at("G2", 15 - p - 8 * h, 143 - p - 8 * h), at(m, 512 * p + h, 512 * p + 512, 2), False, p == 7 and h == 1)
-        return [lambda p=p: one(p) for p in range(8)]
+    small = dict(allow_small_or_imprecise_dtypes=True)
+    ms(at("ones"), 1.0)
+    ms(at("onf"), 1.0)
+    ms(at("JR"), 0.0)
+    iota(at("JR", r0=32, r1=33), [[0, 32], [1, 16]], 0, **small)
+    iota(at("JR", r1=1), [[16, 32], [0, 16]], 0, **small)
+    ts(at("JR", r0=32, r1=33), at("JR", r0=32, r1=33), 0.5, None, A.add)
+    ms(at("JR", r0=64, r1=65), 2.0 ** -7)
+    ms(at("JR", r0=96, r1=97), 1.0)
+    ms(at("JL", r1=64), 2.0 ** -16)
+    ms(at("JL", r0=64), -127.5)
+    for b in range(8):
+        ms(at("JL", 128 * b, 128 * b + 128, r0=64, r1=65), 8.0 + b)
+    select(at("Ib"), at("ones", 0, 128), [[-1, 128]], A.is_equal, 0, 1)
+    select(at("WA"), at("ones", 0, 144), [[-16, 9], [1000, 2], [2, 8]], A.is_equal, -1014, 1)
+    select(at("WB"), at("ones", 0, 144), [[-16, 9], [1000, 2], [2, 8]], A.is_equal, -1015, 1)
+    iota(at("ta"), [[-16, 8], [0, 16]], 0, 1, **small)
+    act(at("tb"), at("ta"), AF.Abs, bias=-7.5)
+    act(at("Blk"), at("tb"), AF.Sigmoid, scale=-256.0, bias=2048.0)
+    select(at("R8a", r1=8), at("onf", r1=8), [[1, 128]], A.is_ge, 0, -16)
+    select(at("R8", r1=8), at("R8a", r1=8), [[-1, 128]], A.is_ge, 15, 16)
+    iota(at("ki"), [[0, 1]], 0, 1)
+    iota(at("RI"), [[0, 17], [1, 16]], 0, **small)
+    ms(at("D0"), 2.0 / 16)
+    ms(at("D0", 0, W // 2, 8), 512.0)
+    ms(at("CM", r0=64), 0.0)
+    for i, (lo, hi) in enumerate(((2.0 ** -10, -127.5), (0.0, -256.0), (0.0, -493568.0), (127.0 * 65536 * 128, -0.5))):
+        ms(at("CM", 128 * i, 128 * i + 128, r0=64, r1=65), lo)
+        ms(at("CM", 128 * i, 128 * i + 128, r0=96, r1=97), hi)
+    ms(at("LE", r1=64), 1.0)
+    ms(at("LE", r0=64), -0.5)
+    for c in range(4):
+        ms(at("LE", 128 * c, 128 * c + 128, r0=64, r1=65), 32768.0 * (16 + c))
+    ms(at("as0"), 0)
+    for n, m, v in (("I8", "Ib", -256.0), ("Im", "Ib", -1.0), ("If", "Ib", 65536.0), ("I17", "Ib", -131072.0), ("I16", "Ib", 65536.0), ("I13", "Ib", -8192.0),
+                    ("Bneg", "Blk", -1.0), ("B12", "Blk", 4096.0), ("B8", "Blk", 256.0), ("Blkf", "Blk", 1.0),
+                    ("B13", "Blk", 8192.0), ("B24", "Blk", -16777216.0), ("B2", "Blk", 2.0)):
+        act(at(n), at(m), scale=v)
+    ts(at("ki2"), at("ki"), 15, None, A.bitwise_and)
+    cp(at("kcf"), at("ki2"))
+    ts(at("ck"), at("kcf"), -4096.0, 128.0 * 65536, A.mult, A.add)
+    ts(at("NP"), at("RI"), at("kcf"), -16384.0, A.not_equal, A.mult)
+    ts(at("thi"), at("thc"), 4032, None, A.bitwise_and)
+    ts(at("tlo"), at("thc"), 63, None, A.bitwise_and)
+    ts(at("nhi"), at("thi"), -1.0, None, A.mult)
+    ts(at("lim0"), at("tlo"), -1.0, -0.5, A.mult, A.add)
+    ts(at("Dhi"), at("Ib"), at("nhi"), None, A.mult)
+    ts(at("Dlo", 0, 128), at("Ib"), at("lim0"), None, A.mult)
+    cp(at("mgf", r1=8), at("mg8", r1=8))
+    mm(at("pK", 0, 1), at("R8", r1=8), at("mgf", r1=8), True, True)
+    ts(at("mgb"), at("pK", 0, 1), -256.0, -128.0, A.mult, A.add)
+    cp(at("P16"), at("gr"))
+    cp(at("Lf"), at("fav"))
+    cp(at("Q16"), at("pa"))
+    for c in range(4):
+        cp(at("S16", c * K, c * K + K), at("Si", c * K, c * K + K))
+    zbank = ("pB", "pW", "pD", "pH", "pJ", "pB", "pW", "pD")
+    for b in range(8):
+        x, z, p = at("X0", 512 * b, 512 * b + 512), at("Z", 512 * b, 512 * b + 512), at(zbank[b])
+        mm(p, at("JL", 128 * b, 128 * b + 128), at("JR"), True, b % 2 == 0)
+        if b % 2 == 0:
+            tt(z, x, p, A.add)
+        else:
+            mm(p, at("Ib"), x, False, True)
+            act(z, p)
 
-    def sgnl(t):
-        act(at("sgl%d" % (t % 2)), at("pD", 0, K), AF.Sign, bias=at("lim%d" % (t % 3)))
+    def lists(t):
+        c = t % 4
+        act(at("Tf"), at("Lf"), off=at("P16", 16 * c, 16 * c + 16))
+        ts(at("Th"), at("Tf"), -2048.0, None, A.add)
+        for w, h in (("WA", 0), ("WB", 128)):
+            group(at("pT", h, h + 128), [(at(w, 8, 136), at("Th", 0, K, 2)), (at(w, 0, 128), at("Th", 1, K, 2))])
+        ts(at("T16"), at("pT", 0, K), 2048.0, None, A.add)
+
+    def column(n):
+        b, s = n // 512, n % 512
+        return (at("JL", 128 * b, 128 * b + 128), at("JR", s, s + K))
 
     def limits(t):
-        a, b = "as%d" % ((t - 1) % 2), "as%d" % (t % 2)
-        tt(at(b), at(a), at("acc"), A.add)
-        ts(at("a63"), at(b), 63, None, A.bitwise_and)
-        ts(at("lim%d" % (t % 3)), at("a63"), -0.5, at("nth"), A.mult, A.add)
+        a, b, n = "as%d" % ((t - 1) % 2), "as%d" % (t % 2), len(PARTS)
+        group(at("pH", K, K + 1), [(at("Blkf"), at("acc", j, j + 1)) for j in range(n * t - n, n * t)])
+        tt(at(b), at(a), at("pH", K, K + 1), A.add)
+        ts(at("a31"), at(b), 31, None, A.bitwise_and)
+        ts(at("lim"), at("a31"), -1.0, at("lim0"), A.mult, A.add)
+        ts(at("Dlo", 128 * t, 128 * t + 128), at("Ib"), at("lim"), None, A.mult)
 
-    def sgnd(t):
-        act(at("sgd%d" % (t % 2)), at("pV", 0, K), AF.Sign, accum=at("acc"))
+    def own(t, a=0, b=K):
+        return at("X%d" % (0 if t < 4 else t), t % 4 * K + a, t % 4 * K + b)
 
-    def lapse_x(t):
-        c, o = cls(t)
-        mm(at("pO", 0, K), at("I256"), at("sgl%d" % (t % 2)), True, True)
-        mm(at("pO", K, 2 * K), at("Ib"), bcol(c), True, True)
-        tt(at("t0"), at("Xb", o, o + K), at("pO", 0, K), A.max)
-        tt(at("x0%d" % t), at("t0"), at("pO", K, 2 * K), A.min)
-        group(at("pB", K, 2 * K), [(at("Ib"), at("x0%d" % t)), (at("BC"), at("JR", 0, K))])
+    def far_start(t):
+        for h in (0, 128):
+            turn(at("pO", 512 + h, 640 + h), own(t, h, h + 128))
+        act(at("bT"), at("pO", 512, 768))
+        for h in (0, 128):
+            turn(at("pO", h, h + 128), at("bT", h, h + 128))
 
-    def xbput(n, x):
-        act(at("Xb", n, n + K), at(x), AF.Identity, bias=128.0)
+    def unturn(p, h, t, scale, stop):
+        for a in (0, 128):
+            mm(at(p, h + a, h + a + 128), at("nl%d" % t, a, a + 128), at(scale), False, stop and a == 128)
 
-    def schain_pe(t):
+    def far_gather(t, a, b, q="S", line=None):
+        out, win, off = at("F%d" % (t % 4), 16 * a, 16 * b), at("X%d" % t), at("S16", t % 4 * K + a, t % 4 * K + b)
+        act(out, win, off=off, line=line) if q == "S" else vgather(out, win, off, line=line)
+
+    def far_sums(t, a, b, last, line=None):
+        f, m = "F%d" % (t % 4), "M%d" % (t % 3)
+        for h in range(a, b, 128):
+            group(at("pD", h, h + 128), [(own(t, h, h + 128), at("Bneg")), (at("ones", 0, 128), at("Dhi"))], stop=False)
+            for p in range(16):
+                mm(at("pD", h + p, h + 128, 16), at(f, 16 * h + p, 16 * h + 2048, 16), at("Bneg", 0, 128, 16), False, False)
+            for p in range(16):
+                lo = 16 * a + (b - a) * p
+                if h == a:
+                    tt(at(m, lo, lo + b - a), at(f, 16 * a + p, 16 * b, 16), at("pO", a, b), A.max, line)
+                mm(at("pD", h + p, h + 128, 16), at(m, lo + h - a, lo + h - a + 128), at("B2", 0, 128, 16), False, False)
+            mm(at("pD", h, h + 128), at("ones", 0, 128), at("Dlo", 128 * t, 128 * t + 128), False, True)
+        if last:
+            act(at("nl%d" % t), at("pD", 0, K), AF.Sigmoid, scale=-256.0)
+
+    def sources(t):
         c, o = cls(t)
         x0 = bcol(c) if t < 4 else at("x0%d" % t)
-        sd, sl = at("sgd%d" % (t % 2)), at("sgl%d" % (t % 2))
-        group(at("pK", K, 2 * K), [(at("LE", 128 * c, 128 * c + 128), at("JR", 0, K)), (at("I12"), sl), (at("I12"), sd)])
-        group(at("pK", 0, K), [(at("If"), at("Fm%d" % (t % 2))), (at("I5"), at("x1_%d" % (t % 2))), (at("I14"), x0), (at("KC"), at("JR", 0, K)), (at("I22"), sd)])
-
-    def schain_v(t):
-        c, o = cls(t)
-        blk = at("Si", o, o + K)
+        w, blk = at("w%d" % t), at("Si", o, o + K)
+        group(at("pK", K, 2 * K), [(at("LE", 128 * c, 128 * c + 128), at("JR", 0, K)), (at("B13"), w)], stop=False)
+        unturn("pK", K, t, "I13", True)
+        group(at("pK", 0, K), [(at("If"), at("Fm%d" % t)), const(3), (at("I17"), at("x1_%d" % t)), (at("I16"), x0), (at("B24"), w)])
         tt(at("s1"), blk, at("pK", K, 2 * K), A.max)
         tt(at("s2"), at("s1"), at("pK", 0, K), A.max)
         ts(blk, at("s2"), 4095, None, A.bitwise_and)
         cp(at("S16" if t < 2 else "ysf", o, o + K), blk)
         if t >= 2:
-            dma("Y", T.ys[:, o:o + K], at("ysf", o, o + K))
+            dma(T.ys[:, o:o + K], at("ysf", o, o + K), 4 * K)
 
-    bg = []
+    def keys_s(a, b):
+        act(at("YS", 8 * a, 8 * b), at("Z"), AF.Identity, bias=-1.0 / 16, off=at("T16", a // 2, b // 2), line="S")
 
-    def run_bg(k):
-        for _ in range(k):
-            if bg:
-                bg.pop(0)()
+    def keys_v(a, b):
+        ys, yv, d0, sc = at("YS", 8 * a, 8 * b), at("YV", 8 * a, 8 * b), at("D0", 8 * a, 8 * b), at("SCN", 8 * a, 8 * b)
+        vgather(yv, at("Z"), at("T16", 128 + a // 2, 128 + b // 2), ys, A.min, "V")
+        emit("V", lambda: g.vector.tensor_tensor_scan(out=sc[0], data0=d0[0], data1=yv[0], initial=512.0, op0=A.add, op1=A.min), [sc], [d0, yv], sc[4])
 
     for t in range(RO):
         c, o = cls(t)
-        late = t >= 4
-        if t >= 1:
-            pre(t)
+        carry(t)
+        lists(t)
+        if t:
             limits(t)
-        if late:
-            fargather(t, 0)
-            fargather(t, 1)
-        for ci, (q, a, b) in enumerate(LATE if late else EARLY):
-            y, d0, sc = at("Y", 16 * a, 16 * b), at("D0", 0, 16 * (b - a)), at("SCN", 16 * a, 16 * b)
-            gather(q, y, at("Z"), at("T16", a, b))
-            if t == 0 and ci == 0:
-                consts1()
-                pre(0)
-                cp(at("S16", 0, K), at("Si", 0, K))
-            if not late and ci == 0:
-                run_bg(EBG[0])
-            if late and ci == 1:
-                if t == 4:
-                    farstart(3)
-                    bg.extend(farops(3))
-                    run_bg(99)
-                    sgnl(3)
-                else:
-                    schain_pe(4)
-                    schain_v(4)
-                farstart(t)
-                bg.extend(farops(t))
-                run_bg(LBG[0])
-            if t == 4 and ci == 4:
-                schain_pe(3)
-                schain_v(3)
-            emit("V", lambda: g.vector.tensor_tensor_scan(out=sc[0], data0=d0[0], data1=y[0], initial=512.0, op0=A.add, op1=A.min), [sc], [d0, y])
-            run_bg((LBG if late else EBG)[ci + 1])
-        run_bg(99)
-        if late:
-            sgnl(t)
-            lapse_x(t)
-        act(at("y0a"), at("Y", 0, W, 16), AF.Identity, bias=12582912.0)
-        act(at("y0b"), at("y0a"), AF.Identity, bias=-12582912.0)
-        gather("S", at("Tf"), at("Lf"), at("P16", 16 * c, 16 * c + 16))
-        x1, xs, R = at("x1_%d" % (t % 2)), at("xs%d" % t), at("SCN", 15, W, 16)
-        ts(at("mi"), R, -0.5, None, A.add)
-        tt(x1, at("mi"), x0col(t), A.min)
-        mm(at("pV", 0, K), at("Bn"), x1, False, True)
-        mm(at("pH", 0, K), at("Blk"), at("y0b"), True, True)
-        tt(at("mx"), x1, at("pV", 0, K), A.max)
-        tt(xs, at("mx"), at("pB", 0, K), A.min)
-        d = 1 + t % (N - 1)
-        nxt, prv = T.cores[(rank + d) % N], T.cores[(rank - d) % N]
-        arr, loc = "arr%d" % t, "loc%d" % t
-        waits("G", loc, [xs], [])
-        rid, pid, _ = topo.addr(nxt)
-        g.remote_dma(out_ap=T["land%d" % t][:], in_ap=xs[0], remote_sem=T.sem[arr], local_sem=T.sem[loc],
-                     pid=pid, routing_id=rid, dma_engine_mask=topo.mask(core, nxt))
-        note("G", loc, loc, len(topo.engines(core, nxt)), [xs], [])
-        note(None, arr, arr, len(topo.engines(prv, core)), [], [at("land%d" % t)])
-        if not late:
-            if t > 0:
-                xbput(o - K, "xs%d" % (t - 1))
-                xbput(told(t - 1), "land%d" % (t - 1))
-            fargather(t, 0)
-            if t > 0:
-                sgnl(t - 1)
-                schain_pe(t - 1)
-            sgnd(t)
-            fargather(t, 1)
+        x0 = at("pB", 0, K)
+        if t < 4:
+            for a, b in KEYS:
+                keys_s(a, b)
+                keys_v(a, b)
+            group(x0, [(at("Ib"), bcol(c)), const(0)])
         else:
-            sgnd(t)
-        if t >= 3:
-            xbput(o, "xs%d" % t)
-            if t < RO - 1:
-                xbput(told(t), "land%d" % t)
+            far_start(t)
+            for i, (what, a, b) in enumerate(LATE):
+                if what in "kK":
+                    (keys_s if what == "k" else keys_v)(a, b)
+                elif what in "fF":
+                    far_gather(t, a, b, *(("S", "S") if what == "f" else ("V", "V")))
+                else:
+                    far_sums(t, a, b, not any(l[0] == "M" for l in LATE[i + 1:]), "V")
+            act(at("ok"), xs_of(t - 4), AF.Identity, bias=2.0 ** -17 - 127.5)
+            group(x0, [(at("Ib"), bcol(c)), const(0)], stop=False)
+            unturn("pB", 0, t, "I8", True)
+            tt(x0, at("ok"), x0, A.max)
+            act(at("x0%d" % t), x0, AF.Identity, bias=127.5)
+        u = [r for r in range(t) if r % 4 == c ^ 1]
+        group(at("pW", 0, K), [(at("Blk"), bcol(c)), (at("Ib"), at("NP", t, t + K))] + ([(at("Bneg"), bcol(c ^ 1)), (at("Blk"), xs_of(u[-1]))] if u else []), stop=False)
+        group(at("pB", K, 2 * K), [(at("Ib"), bcol(c)), const(1)], stop=False)
+        for j, (a, b) in enumerate(PARTS):
+            fm, x1, w = at("Fm%d" % t, a, b), at("x1_%d" % t, a, b), at("w%d" % t, a, b)
+            tt(fm, at("SCN", 8 * a + 7, 8 * b, 8), at("pB", a, b), A.min)
+            ts(x1, fm, MAGIC, 127.0 - MAGIC, A.add, A.add)
+            mm(at("pW", a, b), at("Bneg"), x1, False, b == K)
+            act(w, at("pW", a, b), AF.Sigmoid, bias=at("mgb"), scale=256.0, accum=at("acc", len(PARTS) * t + j, len(PARTS) * t + j + 1))
+            mm(at("pB", K + a, K + b), at("B8"), w, False, b == K)
+            tt(xs_of(t, a, b), x1, at("pB", K + a, K + b), A.max)
+            tell(t, a, b)
+        act(at("y0a"), at("YS", 7, W // 2, 8), AF.Identity, bias=MAGIC)
+        act(at("y0b"), at("y0a"), AF.Identity, bias=-MAGIC)
+        mm(at("pH", 0, K), at("B12"), at("y0b"), True, True)
+        ts(at("hi"), at("pH", 0, K), at("ck"), None, A.add)
+        ts(at("z"), at("hi"), 61440, None, A.bitwise_and)
+        vgather(at("mLQ"), at("Lf"), at("Q16", 16 * c, 16 * c + 16), at("z"), A.max)
+        group(at("pT", K, 2 * K), [(at("Im"), at("Th")), const(2), (at("Blkf"), at("mLQ"))])
+        tt(at("q"), at("pT", K, 2 * K), at("w%d" % t), A.mult)
+        po = at("P16", 16 * c, 16 * c + 16)
+        emit("V", lambda po=po: g.vector.tensor_tensor(out=T.Lf[:].indirect(po[0]), in0=T.q[:], in1=T.Tf[:], op=A.add),
+             [at("Lf")], [at("q"), at("Tf"), po], 60 + K * SCATTER)
         if t < RO - 1:
-            tt(at("Z", o, o + K), xs, at("pJ", 0, K), A.add)
-        cp(at("hi"), at("pH", 0, K))
-        ts(at("h15"), at("hi"), 15, None, A.bitwise_and)
-        ts(at("mask"), at("h15"), at("kcf"), None, A.is_equal)
-        qo, po = at("Q16", 16 * c, 16 * c + 16), at("P16", 16 * c, 16 * c + 16)
-        emit("V", lambda: g.vector.tensor_tensor(out=T.mLQ[:], in0=T.Lf[:].indirect(qo[0]), in1=T.mask[:], op=A.mult), [at("mLQ")], [at("Lf"), qo, at("mask")])
-        group(at("pH", K, 2 * K), [(at("Imf"), at("Tf")), (at("Blkf"), at("mLQ"))])
-        tt(at("w"), at("pV", 0, K), at("THR", t, t + K), A.is_gt)
-        tt(at("Fm%d" % (t % 2)), R, x0col(t), A.min)
-        if t == 0:
-            consts2()
-        if 0 < t < 4:
-            schain_v(t - 1)
-        tt(at("q"), at("pH", K, 2 * K), at("w"), A.mult)
-        emit("V", lambda: g.vector.tensor_tensor(out=T.Lf[:].indirect(po[0]), in0=T.q[:], in1=T.Tf[:], op=A.add), [at("Lf")], [at("q"), at("Tf"), po])
-        if t < RO - 1:
-            tgather(t + 1)
+            group(at("pW", K, 2 * K), [column(o), (at("Ib"), xs_of(t))])
+            act(at("Z", o, o + K), at("pW", K, 2 * K))
             n = told(t)
-            tt(at("Z", n, n + K), at("land%d" % t), at("pJ", K, 2 * K), A.add)
-        if t < 3:
-            farstart(t)
-            bg.extend(farops(t))
-        if t == 2:
-            for lo, hi in ((1280, 1792), (2560, 3328), (3840, 4096)):
-                dma("Y", T.yx[:, lo:hi], at("Xb", lo, hi))
-    dma("Y", T.yl[:], at("Lf"))
-    for lo, hi in ((0, 1280), (1792, 2560), (3584, 3840)):
-        dma("Y", T.yx[:, lo:hi], at("Xb", lo, hi))
-    schain_pe(RO - 1)
+            group(at("pJ", 0, K), [column(n)])
+            for a, b in PARTS:
+                tt(at("Z", n + a, n + b), land_of(t, a, b), at("pJ", a, b), A.add)
+        for r in {0: [0], 1: [1], 2: [2], 4: [4, 3], 5: [5]}.get(t, ()):
+            if r < 4:
+                far_start(r)
+                for a in range(0, K, PIECE):
+                    far_gather(r, a, a + PIECE)
+                far_sums(r, 0, K, True)
+            sources(r)
+    dma(T.yl[:], at("Lf"), 4 * NS)
+    dma(T.yx[:, K:2 * K], at("xs5"), 2 * K)
     n = told(RO - 1)
-    xbput(n, "land%d" % (RO - 1))
-    dma("Y", T.yx[:, n:n + K], at("Xb", n, n + K))
-    schain_v(RO - 1)
+    dma(T.yx[:, n:n + K], at("land5"), 2 * K)
+    for i in in_order(calls):
+        calls[i][1]()
     for s, n in count.items():
         if n and clk["Y"].get(s, 0) < n:
             g.sync.wait_ge(T.sem[s], n)

@@ -3,24 +3,26 @@ import comms_topo
 
 K, W, V, NS, RO = 256, 4096, 1024, 896, 6
 MAGIC = 12582912.0
-KEYS = ((0, 24), (24, 64), (64, 120), (120, 192), (192, 256))
+EARLY = (("k", 0, 24), ("K", 0, 24), ("k", 24, 64), ("K", 24, 64), ("k", 64, 120), ("K", 64, 120), ("k", 120, 192), ("K", 120, 192),
+         ("k", 192, 256), ("K", 192, 256), ("H", 0, 0))
+FIRST = 0
 PARTS = ((0, 256),)
 PIECE = 32
-LATE = (("F", 0, 64), ("k", 0, 24), ("k", 24, 64), ("k", 64, 120), ("K", 0, 24), ("K", 24, 64), ("f", 64, 128), ("K", 64, 120),
-        ("k", 120, 192), ("M", 0, 128), ("f", 128, 256), ("K", 120, 192), ("k", 192, 256), ("M", 128, 256), ("K", 192, 256))
-GATHER, SCATTER, PE, WAKE, DMA, HOP = 1.56, 3.8, 0.75, 80, 2000, 4300
+LATE = (("F", 0, 32), ("f", 32, 128), ("k", 0, 40), ("k", 40, 96), ("M", 0, 128), ("K", 0, 40), ("f", 128, 256), ("K", 40, 96),
+        ("k", 96, 176), ("M", 128, 256), ("K", 96, 176), ("k", 176, 256), ("K", 176, 256), ("H", 0, 0))
+SLACK = 300
+GATHER, SCATTER, PE, WAKE, DMA, HOP = 1.56, 3.8, 0.5, 300, 1000, 2800
 BF, HF, F3, I3, U1 = "bfloat16", "float16", "float32", "int32", "uint16"
 BANKS = ("pB", "pW", "pD", "pK", "pT", "pH", "pJ", "pO")
 _B = {"gr": (64, I3), "pa": (64, I3), "P16": (64, U1), "Q16": (64, U1), "fav": (NS, I3), "Lf": (NS, F3),
       "Si": (V, I3), "S16": (V, U1), "T16": (K, U1), "ysf": (V, F3), "D0": (W // 2, BF), "RI": (272, BF), "NP": (272, BF),
       "JR": (512, BF), "JL": (1024, BF), "LE": (512, BF), "CM": (512, BF), "acc": (RO * len(PARTS), F3)}
 for _d, _w, _l in ((BF, W, "X0 X1 X2 X3 X4 X5 F0 F1 F2 F3 M0 M1 M2"), (F3, W, "Z"), (F3, W // 2, "YS YV SCN"), (I3, K, "hi z s2"),
-                   (F3, K, "Tf mLQ q s1 ok y0a " + " ".join("Fm%d" % _t for _t in range(RO))), (HF, K, "Th"),
-                   (BF, K, "x04 x05 ones bT xs5 land5 y0b"),
-                   (BF, K, " ".join("x1_%d w%d nl%d" % (_t, _t, _t) for _t in range(RO))),
-                   (I3, 1, "thc mg8 as0 as1 a31 ki ki2 thi tlo"),
-                   (F3, 1, "mgf mgb kcf ck nhi lim lim0"),
-                   (BF, 128, "Ib Im ta tb Blk Bneg B2 B8 B12 B13 B24 I17 I16 I13 I8 Dhi"), (BF, 128 * RO, "Dlo"),
+                   (F3, K, "Tf mLQ q s1 ok y0a"), (F3, K * RO, "Fm"), (HF, K, "Th"),
+                   (BF, K, "x04 x05 ones bT xs5 land5 y0b mx sg"), (BF, K * RO, "x1 w nl"),
+                   (I3, 1, "thc mg8 as0 as1 a31 ki ki2 thi tlo mgi mhi mlo"),
+                   (F3, 1, "mgf kcf ck nhi lim lim0 k0 k1 ma mb mc"),
+                   (BF, 128, "Ib Im ta tb Blk Bneg MG B2 B9 B9n B12 B13 B24 I17 I16 I13 I8 Dhi"), (BF, 128 * RO, "Dlo"),
                    (BF, 144, "WA WB"), (F3, 128, "If Blkf R8 R8a onf")):
     for _n in _l.split():
         _B[_n] = (_w, _d)
@@ -62,13 +64,14 @@ def in_order(calls):
         while moved:
             moved = False
             for res, d in need:
-                for a, b in busy.get(res, ()):
-                    if a < t + d and t < b:
-                        t, moved = b, True
+                for a, b, by in busy.get(res, ()):
+                    gap = WAKE if res in BANKS and by != q else 0
+                    if a < t + d + gap and t < b + gap:
+                        t, moved = b + gap, True
         start[i] = t
         for res, d in need:
-            busy[res] = sorted(busy.get(res, []) + [(t, t + d)])
-    return sorted(start, key=lambda i: (start[i], i))
+            busy[res] = sorted(busy.get(res, []) + [(t, t + d, q)])
+    return sorted((t, i) for i, t in start.items())
 
 
 def rank_program(g, core, T, topo):
@@ -79,7 +82,7 @@ def rank_program(g, core, T, topo):
     queue = {"V": g.vector, "S": g.scalar, "P": g.tensor, "G": g, "Y": g.sync}
     count = {"eV": 0, "eS": 0, "eP": 0, "eG": 0}
     clk = {q: {} for q in queue}
-    hist = {}
+    hist, done, now = {}, {}, [0, 0]
     calls = []
 
     def at(name, c0=0, c1=None, step=1, r0=0, r1=128):
@@ -98,6 +101,11 @@ def rank_program(g, core, T, topo):
                         continue
                     if clk[q].get(rsem, 0) < rn and (rsem not in cand or cand[rsem][0] < rn):
                         cand[rsem] = (rn, rclk)
+        for s in cand:
+            for n, end, rc in done.get(s, ())[cand[s][0]:]:
+                if end + WAKE + (0 if s == "e" + q else SLACK) > now[0]:
+                    break
+                cand[s] = (n, rc)
         for s in list(cand):
             n = cand[s][0]
             if not any(o != s and cand[o][1].get(s, 0) >= n for o in cand):
@@ -110,6 +118,8 @@ def rank_program(g, core, T, topo):
         count[sem] = n
         snap = dict(clk[q]) if q else {}
         snap[sem] = n
+        if me in queue:
+            done.setdefault(sem, []).append((n, now[1], snap))
         for w, regs in ((True, outs), (False, ins)):
             for (_, name, lo, hi, _) in regs:
                 keep = [r for r in hist.get(name, ()) if not (lo <= r[0] and r[1] <= hi and (w or (r[3] == me and not r[2])))]
@@ -141,12 +151,12 @@ def rank_program(g, core, T, topo):
         rate = half(out, a, b) * (1 if a[1] in BANKS or b[1] in BANKS else 2)
         emit("V", lambda: g.vector.tensor_tensor(out=out[0], in0=a[0], in1=b[0], op=op), [out], [a, b], out[4] * rate, line)
 
-    def ts(out, a, s1, s2, op0, op1=None):
+    def ts(out, a, s1, s2, op0, op1=None, line=None):
         ins = [a] + [s for s in (s1, s2) if isinstance(s, tuple)]
         v1 = s1[0] if isinstance(s1, tuple) else s1
         v2 = s2[0] if isinstance(s2, tuple) else s2
         kw = {} if op1 is None else {"op1": op1}
-        emit("V", lambda: g.vector.tensor_scalar(out=out[0], in0=a[0], scalar1=v1, scalar2=v2, op0=op0, **kw), [out], ins, out[4] * half(out, a))
+        emit("V", lambda: g.vector.tensor_scalar(out=out[0], in0=a[0], scalar1=v1, scalar2=v2, op0=op0, **kw), [out], ins, out[4] * half(out, a), line)
 
     def cp(out, a):
         emit("V", lambda: g.vector.tensor_copy(out=out[0], in_=a[0]), [out], [a], out[4] * half(out, a))
@@ -204,6 +214,9 @@ def rank_program(g, core, T, topo):
     def told(t):
         return (1 + t % (N - 1)) * V + t % 4 * K
 
+    def of(name, t, a=0, b=K):
+        return at(name, t * K + a, t * K + b)
+
     def bcol(c, a=0, b=K):
         return at("X0", c * K + a, c * K + b)
 
@@ -224,8 +237,8 @@ def rank_program(g, core, T, topo):
 
     loads = [(at("gr"), T.grant[:]), (at("fav"), T.favor[:])] + [(at("X0", V * i, V * i + V), T.base[:, V * i:V * i + V]) for i in range(N)]
     loads += [(at("Si", 0, K), T.src[:, 0:K]), (at("pa"), T.part[:]), (at("mg8", r1=8), T.mg[:]), (at("thc"), T.th[:]), (at("Si", K, V), T.src[:, K:V])]
-    for to, of in loads:
-        dma(to, of, int(to[4] * 4 * half(to)), "loads")
+    for to, hbm in loads:
+        dma(to, hbm, int(to[4] * 4 * half(to)), "loads")
 
     small = dict(allow_small_or_imprecise_dtypes=True)
     ms(at("ones"), 1.0)
@@ -245,7 +258,8 @@ def rank_program(g, core, T, topo):
     select(at("WB"), at("ones", 0, 144), [[-16, 9], [1000, 2], [2, 8]], A.is_equal, -1015, 1)
     iota(at("ta"), [[-16, 8], [0, 16]], 0, 1, **small)
     act(at("tb"), at("ta"), AF.Abs, bias=-7.5)
-    act(at("Blk"), at("tb"), AF.Sigmoid, scale=-256.0, bias=2048.0)
+    act(at("ta"), at("tb"), AF.Sign, scale=-1.0, bias=8.0)
+    act(at("Blk"), at("ta"), AF.Relu)
     select(at("R8a", r1=8), at("onf", r1=8), [[1, 128]], A.is_ge, 0, -16)
     select(at("R8", r1=8), at("R8a", r1=8), [[-1, 128]], A.is_ge, 15, 16)
     iota(at("ki"), [[0, 1]], 0, 1)
@@ -253,22 +267,22 @@ def rank_program(g, core, T, topo):
     ms(at("D0"), 2.0 / 16)
     ms(at("D0", 0, W // 2, 8), 512.0)
     ms(at("CM", r0=64), 0.0)
-    for i, (lo, hi) in enumerate(((2.0 ** -10, -127.5), (0.0, -256.0), (0.0, -493568.0), (127.0 * 65536 * 128, -0.5))):
+    for i, (lo, hi) in enumerate(((2.0 ** -10, -127.5), (0.0, -128.0), (0.0, -493568.0), (127.0 * 65536 * 128, -0.5))):
         ms(at("CM", 128 * i, 128 * i + 128, r0=64, r1=65), lo)
         ms(at("CM", 128 * i, 128 * i + 128, r0=96, r1=97), hi)
     ms(at("LE", r1=64), 1.0)
     ms(at("LE", r0=64), -0.5)
     for c in range(4):
-        ms(at("LE", 128 * c, 128 * c + 128, r0=64, r1=65), 32768.0 * (16 + c))
+        ms(at("LE", 128 * c, 128 * c + 128, r0=64, r1=65), 32768.0 * c)
     ms(at("as0"), 0)
-    for n, m, v in (("I8", "Ib", -256.0), ("Im", "Ib", -1.0), ("If", "Ib", 65536.0), ("I17", "Ib", -131072.0), ("I16", "Ib", 65536.0), ("I13", "Ib", -8192.0),
-                    ("Bneg", "Blk", -1.0), ("B12", "Blk", 4096.0), ("B8", "Blk", 256.0), ("Blkf", "Blk", 1.0),
+    for n, m, v in (("I8", "Ib", -128.0), ("Im", "Ib", -1.0), ("If", "Ib", 65536.0), ("I17", "Ib", -131072.0), ("I16", "Ib", 65536.0), ("I13", "Ib", -4096.0),
+                    ("Bneg", "Blk", -1.0), ("B12", "Blk", 4096.0), ("B9", "Blk", 512.0), ("B9n", "Blk", -512.0), ("Blkf", "Blk", 1.0),
                     ("B13", "Blk", 8192.0), ("B24", "Blk", -16777216.0), ("B2", "Blk", 2.0)):
         act(at(n), at(m), scale=v)
     ts(at("ki2"), at("ki"), 15, None, A.bitwise_and)
     cp(at("kcf"), at("ki2"))
     ts(at("ck"), at("kcf"), -4096.0, 128.0 * 65536, A.mult, A.add)
-    ts(at("NP"), at("RI"), at("kcf"), -16384.0, A.not_equal, A.mult)
+    ts(at("NP"), at("RI"), at("kcf"), -2.0 ** 23, A.not_equal, A.mult)
     ts(at("thi"), at("thc"), 4032, None, A.bitwise_and)
     ts(at("tlo"), at("thc"), 63, None, A.bitwise_and)
     ts(at("nhi"), at("thi"), -1.0, None, A.mult)
@@ -277,7 +291,15 @@ def rank_program(g, core, T, topo):
     ts(at("Dlo", 0, 128), at("Ib"), at("lim0"), None, A.mult)
     cp(at("mgf", r1=8), at("mg8", r1=8))
     mm(at("pK", 0, 1), at("R8", r1=8), at("mgf", r1=8), True, True)
-    ts(at("mgb"), at("pK", 0, 1), -256.0, -128.0, A.mult, A.add)
+    cp(at("mgi"), at("pK", 0, 1))
+    ts(at("mhi"), at("mgi"), 4032, None, A.bitwise_and)
+    ts(at("mlo"), at("mgi"), 63, None, A.bitwise_and)
+    ts(at("k0"), at("kcf"), 0.0, -512.0, A.is_equal, A.mult)
+    ts(at("k1"), at("kcf"), 1.0, -512.0, A.is_equal, A.mult)
+    ts(at("ma"), at("mhi"), at("k0"), None, A.mult)
+    ts(at("mb"), at("mlo"), 0.5, at("k1"), A.add, A.mult)
+    ts(at("mc"), at("ma"), at("mb"), None, A.add)
+    ts(at("MG"), at("Blk"), at("mc"), None, A.mult)
     cp(at("P16"), at("gr"))
     cp(at("Lf"), at("fav"))
     cp(at("Q16"), at("pa"))
@@ -296,7 +318,9 @@ def rank_program(g, core, T, topo):
     def lists(t):
         c = t % 4
         act(at("Tf"), at("Lf"), off=at("P16", 16 * c, 16 * c + 16))
-        ts(at("Th"), at("Tf"), -2048.0, None, A.add)
+        po = at("P16", 16 * c, 16 * c + 16)
+        emit("V", lambda: g.vector.tensor_scalar(out=T.Th[:], in0=T.Lf[:].indirect(po[0]), scalar1=-2048.0, scalar2=None, op0=A.add),
+             [at("Th")], [at("Lf"), po], 60 + K * GATHER)
         for w, h in (("WA", 0), ("WB", 128)):
             group(at("pT", h, h + 128), [(at(w, 8, 136), at("Th", 0, K, 2)), (at(w, 0, 128), at("Th", 1, K, 2))])
         ts(at("T16"), at("pT", 0, K), 2048.0, None, A.add)
@@ -325,7 +349,7 @@ def rank_program(g, core, T, topo):
 
     def unturn(p, h, t, scale, stop):
         for a in (0, 128):
-            mm(at(p, h + a, h + a + 128), at("nl%d" % t, a, a + 128), at(scale), False, stop and a == 128)
+            mm(at(p, h + a, h + a + 128), of("nl", t, a, a + 128), at(scale), False, stop and a == 128)
 
     def far_gather(t, a, b, q="S", line=None):
         out, win, off = at("F%d" % (t % 4), 16 * a, 16 * b), at("X%d" % t), at("S16", t % 4 * K + a, t % 4 * K + b)
@@ -344,15 +368,15 @@ def rank_program(g, core, T, topo):
                 mm(at("pD", h + p, h + 128, 16), at(m, lo + h - a, lo + h - a + 128), at("B2", 0, 128, 16), False, False)
             mm(at("pD", h, h + 128), at("ones", 0, 128), at("Dlo", 128 * t, 128 * t + 128), False, True)
         if last:
-            act(at("nl%d" % t), at("pD", 0, K), AF.Sigmoid, scale=-256.0)
+            act(of("nl", t), at("pD", 0, K), AF.Sign, scale=-1.0)
 
     def sources(t):
         c, o = cls(t)
         x0 = bcol(c) if t < 4 else at("x0%d" % t)
-        w, blk = at("w%d" % t), at("Si", o, o + K)
+        w, blk = of("w", t), at("Si", o, o + K)
         group(at("pK", K, 2 * K), [(at("LE", 128 * c, 128 * c + 128), at("JR", 0, K)), (at("B13"), w)], stop=False)
         unturn("pK", K, t, "I13", True)
-        group(at("pK", 0, K), [(at("If"), at("Fm%d" % t)), const(3), (at("I17"), at("x1_%d" % t)), (at("I16"), x0), (at("B24"), w)])
+        group(at("pK", 0, K), [(at("If"), of("Fm", t)), const(3), (at("I17"), of("x1", t)), (at("I16"), x0), (at("B24"), w)])
         tt(at("s1"), blk, at("pK", K, 2 * K), A.max)
         tt(at("s2"), at("s1"), at("pK", 0, K), A.max)
         ts(blk, at("s2"), 4095, None, A.bitwise_and)
@@ -361,12 +385,27 @@ def rank_program(g, core, T, topo):
             dma(T.ys[:, o:o + K], at("ysf", o, o + K), 4 * K)
 
     def keys_s(a, b):
-        act(at("YS", 8 * a, 8 * b), at("Z"), AF.Identity, bias=-1.0 / 16, off=at("T16", a // 2, b // 2), line="S")
+        ys, off = at("YS", 8 * a, 8 * b), at("T16", a // 2, b // 2)
+        if b <= FIRST:
+            emit("V", lambda: g.vector.tensor_scalar(out=ys[0], in0=T.Z[:].indirect(off[0]), scalar1=-1.0 / 16, scalar2=None, op0=A.add),
+                 [ys], [at("Z"), off], 60 + ys[4] * GATHER, "V")
+        else:
+            act(ys, at("Z"), AF.Identity, bias=-1.0 / 16, off=off, line="S")
 
     def keys_v(a, b):
         ys, yv, d0, sc = at("YS", 8 * a, 8 * b), at("YV", 8 * a, 8 * b), at("D0", 8 * a, 8 * b), at("SCN", 8 * a, 8 * b)
         vgather(yv, at("Z"), at("T16", 128 + a // 2, 128 + b // 2), ys, A.min, "V")
-        emit("V", lambda: g.vector.tensor_tensor_scan(out=sc[0], data0=d0[0], data1=yv[0], initial=512.0, op0=A.add, op1=A.min), [sc], [d0, yv], sc[4])
+        emit("V", lambda: g.vector.tensor_tensor_scan(out=sc[0], data0=d0[0], data1=yv[0], initial=512.0, op0=A.add, op1=A.min), [sc], [d0, yv], sc[4], "scans")
+
+    def entry(t):
+        c = t % 4
+        act(at("y0a"), at("YS", 7, W // 2, 8), AF.Identity, bias=MAGIC, line="S")
+        act(at("y0b"), at("y0a"), AF.Identity, bias=-MAGIC, line="S")
+        mm(at("pH", 0, K), at("B12"), at("y0b"), True, True)
+        ts(at("hi"), at("pH", 0, K), at("ck"), None, A.add, line="V")
+        ts(at("z"), at("hi"), 61440, None, A.bitwise_and, line="V")
+        vgather(at("mLQ"), at("Lf"), at("Q16", 16 * c, 16 * c + 16), at("z"), A.max, "V")
+        group(at("pT", K, 2 * K), [(at("Im"), at("Th")), const(2), (at("Blkf"), at("mLQ"))])
 
     for t in range(RO):
         c, o = cls(t)
@@ -375,45 +414,43 @@ def rank_program(g, core, T, topo):
         if t:
             limits(t)
         x0 = at("pB", 0, K)
+        if t >= 4:
+            far_start(t)
+        plan = EARLY if t < 4 else LATE
+        for i, (what, a, b) in enumerate(plan):
+            if what in "kK":
+                (keys_s if what == "k" else keys_v)(a, b)
+            elif what in "fF":
+                far_gather(t, a, b, *(("S", "S") if what == "f" else ("V", "V")))
+            elif what == "M":
+                far_sums(t, a, b, not any(l[0] == "M" for l in plan[i + 1:]), "V")
+            else:
+                entry(t)
         if t < 4:
-            for a, b in KEYS:
-                keys_s(a, b)
-                keys_v(a, b)
             group(x0, [(at("Ib"), bcol(c)), const(0)])
         else:
-            far_start(t)
-            for i, (what, a, b) in enumerate(LATE):
-                if what in "kK":
-                    (keys_s if what == "k" else keys_v)(a, b)
-                elif what in "fF":
-                    far_gather(t, a, b, *(("S", "S") if what == "f" else ("V", "V")))
-                else:
-                    far_sums(t, a, b, not any(l[0] == "M" for l in LATE[i + 1:]), "V")
             act(at("ok"), xs_of(t - 4), AF.Identity, bias=2.0 ** -17 - 127.5)
-            group(x0, [(at("Ib"), bcol(c)), const(0)], stop=False)
-            unturn("pB", 0, t, "I8", True)
+            group(x0, [(at("Ib"), bcol(c)), const(1)], stop=False)
+            unturn("pB", 0, t, "I8", False)
+            group(x0, [const(0)], start=False)
             tt(x0, at("ok"), x0, A.max)
             act(at("x0%d" % t), x0, AF.Identity, bias=127.5)
         u = [r for r in range(t) if r % 4 == c ^ 1]
-        group(at("pW", 0, K), [(at("Blk"), bcol(c)), (at("Ib"), at("NP", t, t + K))] + ([(at("Bneg"), bcol(c ^ 1)), (at("Blk"), xs_of(u[-1]))] if u else []), stop=False)
-        group(at("pB", K, 2 * K), [(at("Ib"), bcol(c)), const(1)], stop=False)
+        cut = [(at("B9"), bcol(c)), (at("MG"), at("ones"))] + ([(at("B9n"), bcol(c ^ 1)), (at("B9"), xs_of(u[-1]))] if u else [])
+        group(at("pJ", K, 2 * K), cut, stop=False)
+        group(at("pW", 0, K), cut + [(at("Ib"), at("NP", t, t + K))], stop=False)
         for j, (a, b) in enumerate(PARTS):
-            fm, x1, w = at("Fm%d" % t, a, b), at("x1_%d" % t, a, b), at("w%d" % t, a, b)
+            fm, x1, w = of("Fm", t, a, b), of("x1", t, a, b), of("w", t, a, b)
             tt(fm, at("SCN", 8 * a + 7, 8 * b, 8), at("pB", a, b), A.min)
             ts(x1, fm, MAGIC, 127.0 - MAGIC, A.add, A.add)
-            mm(at("pW", a, b), at("Bneg"), x1, False, b == K)
-            act(w, at("pW", a, b), AF.Sigmoid, bias=at("mgb"), scale=256.0, accum=at("acc", len(PARTS) * t + j, len(PARTS) * t + j + 1))
-            mm(at("pB", K + a, K + b), at("B8"), w, False, b == K)
-            tt(xs_of(t, a, b), x1, at("pB", K + a, K + b), A.max)
+            mm(at("pJ", K + a, K + b), at("B9n"), x1, False, b == K)
+            mm(at("pW", a, b), at("B9n"), x1, False, b == K)
+            tt(at("mx", a, b), x1, at("pJ", K + a, K + b), A.max)
+            tt(xs_of(t, a, b), at("mx", a, b), bcol(c, a, b), A.min)
             tell(t, a, b)
-        act(at("y0a"), at("YS", 7, W // 2, 8), AF.Identity, bias=MAGIC)
-        act(at("y0b"), at("y0a"), AF.Identity, bias=-MAGIC)
-        mm(at("pH", 0, K), at("B12"), at("y0b"), True, True)
-        ts(at("hi"), at("pH", 0, K), at("ck"), None, A.add)
-        ts(at("z"), at("hi"), 61440, None, A.bitwise_and)
-        vgather(at("mLQ"), at("Lf"), at("Q16", 16 * c, 16 * c + 16), at("z"), A.max)
-        group(at("pT", K, 2 * K), [(at("Im"), at("Th")), const(2), (at("Blkf"), at("mLQ"))])
-        tt(at("q"), at("pT", K, 2 * K), at("w%d" % t), A.mult)
+            act(at("sg", a, b), at("pW", a, b), AF.Sign)
+            act(w, at("sg", a, b), AF.Relu, accum=at("acc", len(PARTS) * t + j, len(PARTS) * t + j + 1))
+        tt(at("q"), at("pT", K, 2 * K), of("w", t), A.mult)
         po = at("P16", 16 * c, 16 * c + 16)
         emit("V", lambda po=po: g.vector.tensor_tensor(out=T.Lf[:].indirect(po[0]), in0=T.q[:], in1=T.Tf[:], op=A.add),
              [at("Lf")], [at("q"), at("Tf"), po], 60 + K * SCATTER)
@@ -435,7 +472,8 @@ def rank_program(g, core, T, topo):
     dma(T.yx[:, K:2 * K], at("xs5"), 2 * K)
     n = told(RO - 1)
     dma(T.yx[:, n:n + K], at("land5"), 2 * K)
-    for i in in_order(calls):
+    for start, i in in_order(calls):
+        now[:] = start, start + calls[i][4]
         calls[i][1]()
     for s, n in count.items():
         if n and clk["Y"].get(s, 0) < n:

@@ -3,27 +3,39 @@ import comms_topo
 
 K, W, V, NS, RO = 256, 4096, 1024, 896, 6
 MAGIC = 12582912.0
-EARLY = (("k", 0, 24), ("K", 0, 24), ("k", 24, 64), ("K", 24, 64), ("k", 64, 120), ("K", 64, 120), ("k", 120, 192), ("K", 120, 192),
-         ("k", 192, 256), ("K", 192, 256), ("H", 0, 0))
-FIRST = 0
+EARLY = (("v", 0, 40), ("k", 40, 112), ("k", 112, 192), ("K", 0, 40), ("K", 40, 112), ("K", 112, 192), ("a", 192, 256), ("H", 0, 0))
 PARTS = ((0, 256),)
-PIECE = 32
-LATE = (("F", 0, 32), ("f", 32, 128), ("k", 0, 40), ("k", 40, 96), ("M", 0, 128), ("K", 0, 40), ("f", 128, 256), ("K", 40, 96),
-        ("k", 96, 176), ("M", 128, 256), ("K", 96, 176), ("k", 176, 256), ("K", 176, 256), ("H", 0, 0))
-SLACK = 300
+PIECE = 16
+LATE = (("F", 0, 16), ("f", 16, 128), ("f", 128, 256), ("p", 0, 0), ("v", 0, 64), ("v", 64, 128), ("K", 0, 64), ("K", 64, 128), ("M", 0, 128),
+        ("M", 128, 256), ("k", 128, 192), ("k", 192, 256), ("n", 0, 0), ("K", 128, 192), ("K", 192, 256), ("H", 0, 0))
 GATHER, SCATTER, PE, WAKE, DMA, HOP = 1.56, 3.8, 0.5, 300, 1000, 2800
 BF, HF, F3, I3, U1 = "bfloat16", "float16", "float32", "int32", "uint16"
+CONST = {"column": (2.0 ** -16, 2.0 ** -17, 1.0, -127.5), "key": (0, 2.0 ** -17, 0, -127.5), "less": (0, -256.0, 0, 0), "rest": (0, -493568.0, 0, 0),
+         "flag": (0, 16384.0, 127.0 * 65536 * 128, -0.5)}
+CONST.update({"own%d" % _c: (1.0, 256.0 * (_c + 16), 0, 0) for _c in range(4)})
+CONST.update({"over%d" % _c: (-1.0, 256.0 * (48 - _c), 127.0 * 65536 * 128, -0.5) for _c in range(4)})
+YP = (0, 1, 2, 3)
+TH = ()
+ZV = (0, 1, 2, 3, 4)
+ROOM = 1.0
+GATE = 1
+SV = (2, 3, 4, 5)
+XV = (1, 2, 3)
+CONST.update({"told%d" % _t: (0, (14 + 4 * (1 + _t % 3) + _t % 4) / 256, 0, 0) for _t in range(RO - 1)})
+SCALED = (("Im", "Ib", -1.0), ("I8n", "Ib", -256.0), ("I13n", "Ib", -8192.0), ("I49", "Ib", 49152.0), ("I49n", "Ib", -49152.0),
+          ("I16n", "Ib", -65536.0), ("If", "Ib", 1.0), ("I16f", "Ib", 65536.0), ("Bneg", "Blk", -1.0),
+          ("B2", "Blk", 2.0), ("B8", "Blk", 256.0), ("B12", "Blk", 4096.0), ("B53n", "Blk", -53248.0), ("I13", "Ib", 8192.0), ("B9", "Blk", 512.0), ("B9n", "Blk", -512.0), ("B53", "Blk", 53248.0), ("Bf", "Blk", 1.0),
+          ("R0n", "R0", -1.0), ("B12f", "Blk", 4096.0))
 BANKS = ("pB", "pW", "pD", "pK", "pT", "pH", "pJ", "pO")
 _B = {"gr": (64, I3), "pa": (64, I3), "P16": (64, U1), "Q16": (64, U1), "fav": (NS, I3), "Lf": (NS, F3),
-      "Si": (V, I3), "S16": (V, U1), "T16": (K, U1), "ysf": (V, F3), "D0": (W // 2, BF), "RI": (272, BF), "NP": (272, BF),
-      "JR": (512, BF), "JL": (1024, BF), "LE": (512, BF), "CM": (512, BF), "acc": (RO * len(PARTS), F3)}
-for _d, _w, _l in ((BF, W, "X0 X1 X2 X3 X4 X5 F0 F1 F2 F3 M0 M1 M2"), (F3, W, "Z"), (F3, W // 2, "YS YV SCN"), (I3, K, "hi z s2"),
-                   (F3, K, "Tf mLQ q s1 ok y0a"), (F3, K * RO, "Fm"), (HF, K, "Th"),
-                   (BF, K, "x04 x05 ones bT xs5 land5 y0b mx sg"), (BF, K * RO, "x1 w nl"),
-                   (I3, 1, "thc mg8 as0 as1 a31 ki ki2 thi tlo mgi mhi mlo"),
-                   (F3, 1, "mgf kcf ck nhi lim lim0 k0 k1 ma mb mc"),
-                   (BF, 128, "Ib Im ta tb Blk Bneg MG B2 B9 B9n B12 B13 B24 I17 I16 I13 I8 Dhi"), (BF, 128 * RO, "Dlo"),
-                   (BF, 144, "WA WB"), (F3, 128, "If Blkf R8 R8a onf")):
+      "Si": (V, I3), "S16": (V, U1), "T16": (K, U1), "ysf": (V, F3), "D0": (V, BF), "D1": (V, BF), "RI": (272, BF), "NP": (272, BF),
+      "CM": (128 * len(CONST), BF), "acc": (RO * len(PARTS), F3)}
+for _d, _w, _l in ((BF, W, "X0 X1 X2 X3 X4 X5 F0 F1 F2 F3 M0 M1 M2"), (F3, W, "Z"), (F3, W // 2, "YV"), (F3, 3 * V, "YS SCN"), (I3, K, "hi z"),
+                   (I3, 3 * K, "s2"), (F3, 3 * K, "s1"), (F3, K, "Tf mLQ q ok"), (F3, K * RO, "Fm"), (HF, K, "Th"),
+                   (BF, K, "x04 x05 bT xs5 land5"), (BF, 2 * K, "JR"), (BF, K * RO, "x1 w nl"),
+                   (I3, 1, "thc mg8 as0 as1 a31 ki ki2 thi tlo mgi mhi mlo"), (F3, 1, "mgf mgb kcf ck nhi lim lim0 k0 k1 ma mb mc"),
+                   (BF, 128, "Ib ta tb Blk R0 Dhi MG " + " ".join(_n for _n, _, _ in SCALED if _n[-1] != "f")), (BF, 128 * RO, "Dlo"),
+                   (BF, K, "ones mx y0b"), (F3, K, "y0a"), (BF, 144, "WA WB"), (F3, 128, "R8 R8a onf " + " ".join(_n for _n, _, _ in SCALED if _n[-1] == "f"))):
     for _n in _l.split():
         _B[_n] = (_w, _d)
 SCRATCH = {n: ("sbuf", [128, w], d) for n, (w, d) in _B.items()}
@@ -82,18 +94,21 @@ def rank_program(g, core, T, topo):
     queue = {"V": g.vector, "S": g.scalar, "P": g.tensor, "G": g, "Y": g.sync}
     count = {"eV": 0, "eS": 0, "eP": 0, "eG": 0}
     clk = {q: {} for q in queue}
-    hist, done, now = {}, {}, [0, 0]
+    hist, pieces = {}, {}
     calls = []
 
     def at(name, c0=0, c1=None, step=1, r0=0, r1=128):
         c1 = _B[name][0] if c1 is None else c1
         ap = T[name][r0:r1, c0:c1] if step == 1 else T[name][r0:r1, c0:c1:step]
-        return (ap, name, c0, c1, -(-(c1 - c0) // step))
+        return (ap, name, c0, c1, -(-(c1 - c0) // step), range(r0 // 32, (r1 + 31) // 32))
+
+    def rows(regs):
+        return [(r[0], r[1] + str(k)) + r[2:] for r in regs if r[1] in ("JR", "CM") for k in r[5]] + [r for r in regs if r[1] not in ("JR", "CM")]
 
     def waits(q, me, ins, outs):
         cand = {}
         for wr, regs in ((False, ins), (True, outs)):
-            for (_, name, lo, hi, _) in regs:
+            for (_, name, lo, hi, _, _) in regs:
                 for rlo, rhi, rw, rme, rsem, rn, rclk in hist.get(name, ()):
                     if rme == me and me == "P":
                         continue
@@ -101,11 +116,6 @@ def rank_program(g, core, T, topo):
                         continue
                     if clk[q].get(rsem, 0) < rn and (rsem not in cand or cand[rsem][0] < rn):
                         cand[rsem] = (rn, rclk)
-        for s in cand:
-            for n, end, rc in done.get(s, ())[cand[s][0]:]:
-                if end + WAKE + (0 if s == "e" + q else SLACK) > now[0]:
-                    break
-                cand[s] = (n, rc)
         for s in list(cand):
             n = cand[s][0]
             if not any(o != s and cand[o][1].get(s, 0) >= n for o in cand):
@@ -118,31 +128,30 @@ def rank_program(g, core, T, topo):
         count[sem] = n
         snap = dict(clk[q]) if q else {}
         snap[sem] = n
-        if me in queue:
-            done.setdefault(sem, []).append((n, now[1], snap))
         for w, regs in ((True, outs), (False, ins)):
-            for (_, name, lo, hi, _) in regs:
+            for (_, name, lo, hi, _, _) in regs:
                 keep = [r for r in hist.get(name, ()) if not (lo <= r[0] and r[1] <= hi and (w or (r[3] == me and not r[2])))]
                 hist[name] = keep + [(lo, hi, w, me, sem, n, snap)]
 
     def emit(q, f, outs, ins, cost, line=None):
+        outs, ins = rows(outs), rows(ins)
+
         def issue():
-            o = outs + [(None, "gq", 0, 1, 1)] if q == "G" else outs
-            waits(q, q, ins, o)
+            waits(q, q, ins, outs)
             f().then_inc(T.sem["e" + q], 1)
-            note(q, q, "e" + q, count["e" + q] + 1, ins, o)
+            note(q, q, "e" + q, count["e" + q] + 1, ins, outs)
         calls.append((q, issue, outs, ins, max(32 if q == "P" else 64, cost), 0, line))
 
-    def dma(out, in_, size, line=None):
+    def dma(out, in_, size, line=None, q="Y"):
         outs = [out] if isinstance(out, tuple) else []
         ins = [in_] if isinstance(in_, tuple) else []
-        s = "d%d" % sum(c[0] == "Y" for c in calls)
+        s = "d%d" % sum(c[0] != "G" and c[5] > 0 for c in calls)
 
         def issue():
-            waits("Y", s, ins, outs)
-            g.sync.dma_start(out[0] if outs else out, in_[0] if ins else in_).then_inc(T.sem[s], 16)
-            note("Y", s, s, 16, ins, outs)
-        calls.append(("Y", issue, outs, ins, 64, DMA + 500 + size // 2, line))
+            waits(q, s, ins, outs)
+            queue[q].dma_start(out[0] if outs else out, in_[0] if ins else in_).then_inc(T.sem[s], 16)
+            note(q, s, s, 16, ins, outs)
+        calls.append((q, issue, outs, ins, 64, DMA + 300 + size // 3, line))
 
     def half(*regs):
         return 0.5 if all(_B[r[1]][1] in (BF, HF, U1) for r in regs) else 1
@@ -158,29 +167,29 @@ def rank_program(g, core, T, topo):
         kw = {} if op1 is None else {"op1": op1}
         emit("V", lambda: g.vector.tensor_scalar(out=out[0], in0=a[0], scalar1=v1, scalar2=v2, op0=op0, **kw), [out], ins, out[4] * half(out, a), line)
 
-    def cp(out, a):
-        emit("V", lambda: g.vector.tensor_copy(out=out[0], in_=a[0]), [out], [a], out[4] * half(out, a))
+    def cp(out, a, line=None):
+        emit("V", lambda: g.vector.tensor_copy(out=out[0], in_=a[0]), [out], [a], out[4] * half(out, a), line)
 
     def ms(out, c):
         emit("V", lambda: g.vector.memset(out[0], c), [out], [], out[4] * half(out))
 
     def act(out, a, func=AF.Copy, bias=0.0, scale=1.0, accum=None, off=None, line=None):
-        ins = [a] + ([bias] if isinstance(bias, tuple) else []) + ([off] if off else [])
+        ins = [a] + [s for s in (bias, scale, off) if isinstance(s, tuple)]
         kw = {} if accum is None else {"accum_out": accum[0]}
-        b = bias[0] if isinstance(bias, tuple) else bias
+        b, sc = (s[0] if isinstance(s, tuple) else s for s in (bias, scale))
         src = a[0].indirect(off[0]) if off else a[0]
-        emit("S", lambda: g.scalar.activation(out=out[0], in_=src, func=func, bias=b, scale=scale, **kw), [out] + ([accum] if accum else []), ins,
+        emit("S", lambda: g.scalar.activation(out=out[0], in_=src, func=func, bias=b, scale=sc, **kw), [out] + ([accum] if accum else []), ins,
              80 + out[4] * GATHER if off else out[4], line)
 
-    def mm(out, l, r, start, stop):
-        emit("P", lambda: g.tensor.matmul(out=out[0], lhsT=l[0], rhs=r[0], start=start, stop=stop), [out], [l, r], PE * max(64, r[4]) * (1 if half(r) < 1 else 4))
+    def mm(out, l, r, start, stop, gate=(), line=None):
+        emit("P", lambda: g.tensor.matmul(out=out[0], lhsT=l[0], rhs=r[0], start=start, stop=stop), [out], [l, r, *gate], PE * max(64, r[4]) * (1 if half(r) < 1 else 4) * (ROOM if out[1] in ("pD", "pK") else 1), line)
 
-    def group(out, pairs, start=True, stop=True):
+    def group(out, pairs, stop=True, gate=(), line=None):
         for i, (l, r) in enumerate(pairs):
-            mm(out, l, r, start and i == 0, stop and i == len(pairs) - 1)
+            mm(out, l, r, i == 0, stop and i == len(pairs) - 1, gate, line)
 
-    def turn(out, a):
-        emit("P", lambda: g.tensor.transpose(out[0], a[0], T.Ib[:]), [out], [a, at("Ib")], 128 * PE)
+    def turn(out, a, line=None):
+        emit("P", lambda: g.tensor.transpose(out[0], a[0], T.Ib[:]), [out], [a, at("Ib")], 128 * PE, line)
 
     def vgather(out, win, off, b=None, op=None, line=None):
         if b is None:
@@ -211,6 +220,9 @@ def rank_program(g, core, T, topo):
     def cls(t):
         return t % 4, t % 4 * K
 
+    def paired(t):
+        return min([a for what, a, _ in (EARLY if t < 4 else LATE) if what == "a"] + [K])
+
     def told(t):
         return (1 + t % (N - 1)) * V + t % 4 * K
 
@@ -226,8 +238,10 @@ def rank_program(g, core, T, topo):
     def land_of(t, a=0, b=K):
         return at("X%d" % (t + 1), told(t) + a, told(t) + b) if t < RO - 1 else at("land5", a, b)
 
-    def const(i):
-        return (at("CM", 128 * i, 128 * i + 128, r0=64), at("JR", 0, K, r0=64))
+    def const(name, n=K):
+        i, used = list(CONST).index(name), [32 * r for r, v in enumerate(CONST[name]) if v]
+        r = dict(r0=used[0], r1=used[0] + 1) if len(used) == 1 else {}
+        return (at("CM", 128 * i, 128 * i + 128, **r), at("JR", 0, n, **r))
 
     def carry(t):
         o, n = t % 4 * K, told(t)
@@ -244,53 +258,59 @@ def rank_program(g, core, T, topo):
     ms(at("ones"), 1.0)
     ms(at("onf"), 1.0)
     ms(at("JR"), 0.0)
-    iota(at("JR", r0=32, r1=33), [[0, 32], [1, 16]], 0, **small)
-    iota(at("JR", r1=1), [[16, 32], [0, 16]], 0, **small)
-    ts(at("JR", r0=32, r1=33), at("JR", r0=32, r1=33), 0.5, None, A.add)
-    ms(at("JR", r0=64, r1=65), 2.0 ** -7)
-    ms(at("JR", r0=96, r1=97), 1.0)
-    ms(at("JL", r1=64), 2.0 ** -16)
-    ms(at("JL", r0=64), -127.5)
-    for b in range(8):
-        ms(at("JL", 128 * b, 128 * b + 128, r0=64, r1=65), 8.0 + b)
+    iota(at("JR", 0, K, r1=1), [[1, K]], 0, **small)
+    act(at("JR", K, 2 * K, r1=1), at("JR", 0, K, r1=1))
+    for r, v, a in ((32, 1.0, 0), (64, 2.0 ** -7, 0), (96, 1.0, 0), (64, 3 * 2.0 ** -8, K)):
+        ms(at("JR", a, r0=r, r1=r + 1), v)
+    for i, row in enumerate(CONST.values()):
+        one = sum(v != 0 for v in row) == 1
+        for r, v in enumerate(row):
+            if v if one else (r == 0 or v != row[0]):
+                to = at("CM", 128 * i, 128 * i + 128, r0=32 * r, r1=32 * r + 1 if r or one else 128)
+                ms(to, v) if i < 2 else act(to, at("ones", 0, 128, r0=32 * r, r1=32 * r + 1 if r or one else 128), scale=float(v))
+    select(at("R0"), at("ones", 0, 128), [[-16, 8], [0, 16]], A.is_equal, 0, 1)
     select(at("Ib"), at("ones", 0, 128), [[-1, 128]], A.is_equal, 0, 1)
     select(at("WA"), at("ones", 0, 144), [[-16, 9], [1000, 2], [2, 8]], A.is_equal, -1014, 1)
     select(at("WB"), at("ones", 0, 144), [[-16, 9], [1000, 2], [2, 8]], A.is_equal, -1015, 1)
     iota(at("ta"), [[-16, 8], [0, 16]], 0, 1, **small)
     act(at("tb"), at("ta"), AF.Abs, bias=-7.5)
-    act(at("ta"), at("tb"), AF.Sign, scale=-1.0, bias=8.0)
-    act(at("Blk"), at("ta"), AF.Relu)
+    act(at("Blk"), at("tb"), AF.Sigmoid, scale=-256.0, bias=2048.0)
     select(at("R8a", r1=8), at("onf", r1=8), [[1, 128]], A.is_ge, 0, -16)
     select(at("R8", r1=8), at("R8a", r1=8), [[-1, 128]], A.is_ge, 15, 16)
     iota(at("ki"), [[0, 1]], 0, 1)
     iota(at("RI"), [[0, 17], [1, 16]], 0, **small)
     ms(at("D0"), 2.0 / 16)
-    ms(at("D0", 0, W // 2, 8), 512.0)
-    ms(at("CM", r0=64), 0.0)
-    for i, (lo, hi) in enumerate(((2.0 ** -10, -127.5), (0.0, -128.0), (0.0, -493568.0), (127.0 * 65536 * 128, -0.5))):
-        ms(at("CM", 128 * i, 128 * i + 128, r0=64, r1=65), lo)
-        ms(at("CM", 128 * i, 128 * i + 128, r0=96, r1=97), hi)
-    ms(at("LE", r1=64), 1.0)
-    ms(at("LE", r0=64), -0.5)
-    for c in range(4):
-        ms(at("LE", 128 * c, 128 * c + 128, r0=64, r1=65), 32768.0 * c)
+    ms(at("D0", 0, V, 8), 512.0)
+    ms(at("D1"), -1.0 / 16)
+    ms(at("D1", 0, V, 16), 512.0)
     ms(at("as0"), 0)
-    for n, m, v in (("I8", "Ib", -128.0), ("Im", "Ib", -1.0), ("If", "Ib", 65536.0), ("I17", "Ib", -131072.0), ("I16", "Ib", 65536.0), ("I13", "Ib", -4096.0),
-                    ("Bneg", "Blk", -1.0), ("B12", "Blk", 4096.0), ("B9", "Blk", 512.0), ("B9n", "Blk", -512.0), ("Blkf", "Blk", 1.0),
-                    ("B13", "Blk", 8192.0), ("B24", "Blk", -16777216.0), ("B2", "Blk", 2.0)):
+    for n, m, v in SCALED:
         act(at(n), at(m), scale=v)
     ts(at("ki2"), at("ki"), 15, None, A.bitwise_and)
     cp(at("kcf"), at("ki2"))
     ts(at("ck"), at("kcf"), -4096.0, 128.0 * 65536, A.mult, A.add)
-    ts(at("NP"), at("RI"), at("kcf"), -2.0 ** 23, A.not_equal, A.mult)
+    ts(at("NP"), at("RI"), at("kcf"), -16384.0, A.not_equal, A.mult)
     ts(at("thi"), at("thc"), 4032, None, A.bitwise_and)
     ts(at("tlo"), at("thc"), 63, None, A.bitwise_and)
     ts(at("nhi"), at("thi"), -1.0, None, A.mult)
     ts(at("lim0"), at("tlo"), -1.0, -0.5, A.mult, A.add)
-    ts(at("Dhi"), at("Ib"), at("nhi"), None, A.mult)
-    ts(at("Dlo", 0, 128), at("Ib"), at("lim0"), None, A.mult)
+    act(at("Dhi"), at("Ib"), AF.Identity, scale=at("nhi"))
+    act(at("Dlo", 0, 128), at("Ib"), AF.Identity, scale=at("lim0"))
     cp(at("mgf", r1=8), at("mg8", r1=8))
+    cp(at("P16"), at("gr"))
+    cp(at("Lf"), at("fav"))
+    cp(at("Q16"), at("pa"))
+    for c in range(4):
+        cp(at("S16", c * K, c * K + K), at("Si", c * K, c * K + K), None if c else "V")
+
+    def zput(n, x, p, q="S"):
+        z, bias = at("Z", n, n + x[4]), (W + n - 512) / 65536
+        group(p, [const("column", x[4]), (at("Ib"), x)])
+        act(z, p, AF.Identity, bias=bias) if q == "S" else ts(z, p, bias, None, A.add)
+    for b in range(8):
+        zput(512 * b, at("X0", 512 * b, 512 * b + 512), at(("pB", "pW", "pD", "pH", "pJ", "pK")[b % 6]), "SV"[b % 2])
     mm(at("pK", 0, 1), at("R8", r1=8), at("mgf", r1=8), True, True)
+    ts(at("mgb"), at("pK", 0, 1), -256.0, -128.0, A.mult, A.add)
     cp(at("mgi"), at("pK", 0, 1))
     ts(at("mhi"), at("mgi"), 4032, None, A.bitwise_and)
     ts(at("mlo"), at("mgi"), 63, None, A.bitwise_and)
@@ -299,43 +319,31 @@ def rank_program(g, core, T, topo):
     ts(at("ma"), at("mhi"), at("k0"), None, A.mult)
     ts(at("mb"), at("mlo"), 0.5, at("k1"), A.add, A.mult)
     ts(at("mc"), at("ma"), at("mb"), None, A.add)
-    ts(at("MG"), at("Blk"), at("mc"), None, A.mult)
-    cp(at("P16"), at("gr"))
-    cp(at("Lf"), at("fav"))
-    cp(at("Q16"), at("pa"))
-    for c in range(4):
-        cp(at("S16", c * K, c * K + K), at("Si", c * K, c * K + K))
-    zbank = ("pB", "pW", "pD", "pH", "pJ", "pB", "pW", "pD")
-    for b in range(8):
-        x, z, p = at("X0", 512 * b, 512 * b + 512), at("Z", 512 * b, 512 * b + 512), at(zbank[b])
-        mm(p, at("JL", 128 * b, 128 * b + 128), at("JR"), True, b % 2 == 0)
-        if b % 2 == 0:
-            tt(z, x, p, A.add)
-        else:
-            mm(p, at("Ib"), x, False, True)
-            act(z, p)
+    act(at("MG"), at("Blk"), AF.Identity, scale=at("mc"))
 
     def lists(t):
         c = t % 4
         act(at("Tf"), at("Lf"), off=at("P16", 16 * c, 16 * c + 16))
         po = at("P16", 16 * c, 16 * c + 16)
-        emit("V", lambda: g.vector.tensor_scalar(out=T.Th[:], in0=T.Lf[:].indirect(po[0]), scalar1=-2048.0, scalar2=None, op0=A.add),
-             [at("Th")], [at("Lf"), po], 60 + K * GATHER)
-        for w, h in (("WA", 0), ("WB", 128)):
-            group(at("pT", h, h + 128), [(at(w, 8, 136), at("Th", 0, K, 2)), (at(w, 0, 128), at("Th", 1, K, 2))])
-        ts(at("T16"), at("pT", 0, K), 2048.0, None, A.add)
-
-    def column(n):
-        b, s = n // 512, n % 512
-        return (at("JL", 128 * b, 128 * b + 128), at("JR", s, s + K))
+        if t in TH:
+            ts(at("Th"), at("Tf"), -2048.0, None, A.add)
+        else:
+            emit("V", lambda: g.vector.tensor_scalar(out=T.Th[:], in0=T.Lf[:].indirect(po[0]), scalar1=-2048.0, scalar2=None, op0=A.add),
+                 [at("Th")], [at("Lf"), po], 60 + K * GATHER)
+        n = paired(t)
+        for w, h in (("WA", 0), ("WB", n // 2)):
+            group(at("pT", h, h + n // 2), [(at(w, 8, 136), at("Th", 0, n, 2)), (at(w, 0, 128), at("Th", 1, n, 2))])
+        ts(at("T16", 0, n), at("pT", 0, n), 2048.0, None, A.add)
+        if n < K:
+            ts(at("T16", n, K), at("Th", n, K), 2048.0, None, A.add)
 
     def limits(t):
         a, b, n = "as%d" % ((t - 1) % 2), "as%d" % (t % 2), len(PARTS)
-        group(at("pH", K, K + 1), [(at("Blkf"), at("acc", j, j + 1)) for j in range(n * t - n, n * t)])
-        tt(at(b), at(a), at("pH", K, K + 1), A.add)
+        group(at("pH", 0, 1), [(at("Bf"), at("acc", j, j + 1)) for j in range(n * t - n, n * t)])
+        tt(at(b), at(a), at("pH", 0, 1), A.add)
         ts(at("a31"), at(b), 31, None, A.bitwise_and)
         ts(at("lim"), at("a31"), -1.0, at("lim0"), A.mult, A.add)
-        ts(at("Dlo", 128 * t, 128 * t + 128), at("Ib"), at("lim"), None, A.mult)
+        act(at("Dlo", 128 * t, 128 * t + 128), at("Ib"), AF.Identity, scale=at("lim"))
 
     def own(t, a=0, b=K):
         return at("X%d" % (0 if t < 4 else t), t % 4 * K + a, t % 4 * K + b)
@@ -345,7 +353,7 @@ def rank_program(g, core, T, topo):
             turn(at("pO", 512 + h, 640 + h), own(t, h, h + 128))
         act(at("bT"), at("pO", 512, 768))
         for h in (0, 128):
-            turn(at("pO", h, h + 128), at("bT", h, h + 128))
+            turn(at("pO", h, h + 128), at("bT", h, h + 128), "P" if t >= 4 else None)
 
     def unturn(p, h, t, scale, stop):
         for a in (0, 128):
@@ -355,57 +363,90 @@ def rank_program(g, core, T, topo):
         out, win, off = at("F%d" % (t % 4), 16 * a, 16 * b), at("X%d" % t), at("S16", t % 4 * K + a, t % 4 * K + b)
         act(out, win, off=off, line=line) if q == "S" else vgather(out, win, off, line=line)
 
-    def far_sums(t, a, b, last, line=None):
-        f, m = "F%d" % (t % 4), "M%d" % (t % 3)
+    def far_max(t, a, b, line=None):
+        for p in range(16):
+            lo = 16 * a + (b - a) * p
+            tt(at("M%d" % (t % 3), lo, lo + b - a), at("F%d" % (t % 4), 16 * a + p, 16 * b, 16), at("pO", a, b), A.max, line)
+
+    def far_sums(t, a, b, gate=()):
+        f, m, d = "F%d" % (t % 4), "M%d" % (t % 3), "pD" if t < 4 else "pJ"
         for h in range(a, b, 128):
-            group(at("pD", h, h + 128), [(own(t, h, h + 128), at("Bneg")), (at("ones", 0, 128), at("Dhi"))], stop=False)
+            group(at(d, h, h + 128), [(own(t, h, h + 128), at("Bneg")), (at("ones", 0, 128), at("Dhi"))], stop=False, gate=gate, line="P" if t < 4 else None)
             for p in range(16):
-                mm(at("pD", h + p, h + 128, 16), at(f, 16 * h + p, 16 * h + 2048, 16), at("Bneg", 0, 128, 16), False, False)
+                mm(at(d, h + p, h + 128, 16), at(f, 16 * h + p, 16 * h + 2048, 16), at("Bneg", 0, 128, 16), False, False)
             for p in range(16):
-                lo = 16 * a + (b - a) * p
-                if h == a:
-                    tt(at(m, lo, lo + b - a), at(f, 16 * a + p, 16 * b, 16), at("pO", a, b), A.max, line)
-                mm(at("pD", h + p, h + 128, 16), at(m, lo + h - a, lo + h - a + 128), at("B2", 0, 128, 16), False, False)
-            mm(at("pD", h, h + 128), at("ones", 0, 128), at("Dlo", 128 * t, 128 * t + 128), False, True)
-        if last:
-            act(of("nl", t), at("pD", 0, K), AF.Sign, scale=-1.0)
+                mm(at(d, h + p, h + 128, 16), at(m, 16 * h + 128 * p, 16 * h + 128 * p + 128), at("B2", 0, 128, 16), False, False)
+            mm(at(d, h, h + 128), at("ones", 0, 128), at("Dlo", 128 * t, 128 * t + 128), False, True)
+
+    def far_end(t, line=None):
+        act(of("nl", t), at("pD" if t < 4 else "pJ", 0, K), AF.Sigmoid, scale=-256.0, line=line)
 
     def sources(t):
         c, o = cls(t)
         x0 = bcol(c) if t < 4 else at("x0%d" % t)
         w, blk = of("w", t), at("Si", o, o + K)
-        group(at("pK", K, 2 * K), [(at("LE", 128 * c, 128 * c + 128), at("JR", 0, K)), (at("B13"), w)], stop=False)
-        unturn("pK", K, t, "I13", True)
-        group(at("pK", 0, K), [(at("If"), of("Fm", t)), const(3), (at("I17"), of("x1", t)), (at("I16"), x0), (at("B24"), w)])
-        tt(at("s1"), blk, at("pK", K, 2 * K), A.max)
-        tt(at("s2"), at("s1"), at("pK", 0, K), A.max)
-        ts(blk, at("s2"), 4095, None, A.bitwise_and)
+        fm, x1, xs = of("Fm", t), of("x1", t), xs_of(t)
+        both = t in SV
+        favour = [(at("I16f"), fm), const("flag" if both else "over%d" % c), (at("I16n"), x1), (at("I49"), x0), (at("I49n"), xs)]
+        p, s1, s2 = {3: "pD", 5: "pJ"}.get(t, "pK"), of("s1", t % 3), of("s2", t % 3)
+        group(at(p, 0, K), favour + ([] if both else [(at("B53n"), w)]), stop=both, line="P" if t < 3 else None)
+        if not both:
+            unturn(p, 0, t, "I13", True)
+            act(s1, at(p, 0, K), AF.Relu)
+        group(at(p, K, 2 * K), [const("own%d" % c), (at("B53"), w)], stop=False)
+        unturn(p, K, t, "I13n", both)
+        if both:
+            tt(s1, blk, at(p, K, 2 * K), A.max)
+            tt(s2, s1, at(p, 0, K), A.max)
+        else:
+            mm(at(p, K, 2 * K), at("If"), s1, False, True)
+            tt(s2, blk, at(p, K, 2 * K), A.max)
+        ts(blk, s2, 4095, None, A.bitwise_and)
         cp(at("S16" if t < 2 else "ysf", o, o + K), blk)
         if t >= 2:
             dma(T.ys[:, o:o + K], at("ysf", o, o + K), 4 * K)
 
-    def keys_s(a, b):
+    def keys_s(a, b, vector):
         ys, off = at("YS", 8 * a, 8 * b), at("T16", a // 2, b // 2)
-        if b <= FIRST:
+        if vector:
             emit("V", lambda: g.vector.tensor_scalar(out=ys[0], in0=T.Z[:].indirect(off[0]), scalar1=-1.0 / 16, scalar2=None, op0=A.add),
                  [ys], [at("Z"), off], 60 + ys[4] * GATHER, "V")
         else:
             act(ys, at("Z"), AF.Identity, bias=-1.0 / 16, off=off, line="S")
 
-    def keys_v(a, b):
-        ys, yv, d0, sc = at("YS", 8 * a, 8 * b), at("YV", 8 * a, 8 * b), at("D0", 8 * a, 8 * b), at("SCN", 8 * a, 8 * b)
-        vgather(yv, at("Z"), at("T16", 128 + a // 2, 128 + b // 2), ys, A.min, "V")
-        emit("V", lambda: g.vector.tensor_tensor_scan(out=sc[0], data0=d0[0], data1=yv[0], initial=512.0, op0=A.add, op1=A.min), [sc], [d0, yv], sc[4], "scans")
+    def scan(out, steps, y, line):
+        emit("V", lambda: g.vector.tensor_tensor_scan(out=out[0], data0=steps[0], data1=y[0], initial=512.0, op0=A.add, op1=A.min), [out], [steps, y], out[4], line)
+
+    def keys_v(t, a, b):
+        n = paired(t)
+        vgather(at("YV", 8 * a, 8 * b), at("Z"), at("T16", (n + a) // 2, (n + b) // 2), at("YS", 8 * a, 8 * b), A.min, "V")
+        scan(at("SCN", 8 * a, 8 * b), at("D0", 0, 8 * (b - a)), at("YV", 8 * a, 8 * b), "scans")
+
+    def keys_all(t, a, b):
+        lo, hi = 16 * a - 8 * paired(t), 16 * b - 8 * paired(t)
+        act(at("YS", lo, hi), at("Z"), AF.Identity, bias=14.0 / 16, off=at("T16", a, b), line="S")
+        scan(at("SCN", lo, hi), at("D1", 0, hi - lo), at("YS", lo, hi), "scans")
+
+    def ends(name, t, first):
+        n = paired(t)
+        return [(0, n, at(name, 7, 8 * n, 8))] + ([(n, K, at(name, 8 * n + (0 if first else 15), 16 * K - 8 * n, 16))] if n < K else [])
 
     def entry(t):
         c = t % 4
-        act(at("y0a"), at("YS", 7, W // 2, 8), AF.Identity, bias=MAGIC, line="S")
-        act(at("y0b"), at("y0a"), AF.Identity, bias=-MAGIC, line="S")
-        mm(at("pH", 0, K), at("B12"), at("y0b"), True, True)
-        ts(at("hi"), at("pH", 0, K), at("ck"), None, A.add, line="V")
+        if t in YP:
+            mm(at("pH", 0, K), at("R0n"), at("Th"), True, False)
+            for a, b, y in ends("YS", t, True):
+                mm(at("pH", a, b), at("B12f"), y, False, b == K, line="P")
+        else:
+            for a, b, y in ends("YS", t, True):
+                act(at("y0a", a, b), y, AF.Identity, bias=MAGIC, line="S")
+            act(at("y0b"), at("y0a"), AF.Identity, bias=-MAGIC, line="S")
+            mm(at("pH", 0, K), at("B12"), at("y0b"), True, True, line="P")
+        for a, b, y in ends("YS", t, True) if t in YP else [(0, K, 0)]:
+            ts(at("hi", a, b), at("pH", a, b), at("ck"), 65536 * (0 if t not in YP else 0.5 if a == 0 else 0.5 - 15.0 / 16), A.add, A.add, line="V")
         ts(at("z"), at("hi"), 61440, None, A.bitwise_and, line="V")
         vgather(at("mLQ"), at("Lf"), at("Q16", 16 * c, 16 * c + 16), at("z"), A.max, "V")
-        group(at("pT", K, 2 * K), [(at("Im"), at("Th")), const(2), (at("Blkf"), at("mLQ"))])
+        group(at("pT", K, 2 * K), [(at("Im"), at("Th")), const("rest"), (at("Bf"), at("mLQ"))])
 
     for t in range(RO):
         c, o = cls(t)
@@ -416,65 +457,100 @@ def rank_program(g, core, T, topo):
         x0 = at("pB", 0, K)
         if t >= 4:
             far_start(t)
+        if t >= 2:
+            far_sums(t - 2, 0, K, [at("T16")] if GATE else [])
+
         plan = EARLY if t < 4 else LATE
         for i, (what, a, b) in enumerate(plan):
-            if what in "kK":
-                (keys_s if what == "k" else keys_v)(a, b)
+            if what in "kv":
+                keys_s(a, b, what == "v")
+            elif what == "K":
+                keys_v(t, a, b)
+            elif what == "a":
+                keys_all(t, a, b)
             elif what in "fF":
                 far_gather(t, a, b, *(("S", "S") if what == "f" else ("V", "V")))
             elif what == "M":
-                far_sums(t, a, b, not any(l[0] == "M" for l in plan[i + 1:]), "V")
+                far_max(t, a, b, "V")
+                far_sums(t, a, b)
+            elif what == "n":
+                far_end(t, "S")
+            elif what == "p":
+                far_end(t - 2, "S")
             else:
                 entry(t)
+        if t >= 2:
+            if ("p", 0, 0) not in plan:
+                far_end(t - 2, "S")
+            sources(t - 2)
         if t < 4:
-            group(x0, [(at("Ib"), bcol(c)), const(0)])
+            group(x0, [(at("Ib"), bcol(c)), const("key")])
         else:
             act(at("ok"), xs_of(t - 4), AF.Identity, bias=2.0 ** -17 - 127.5)
-            group(x0, [(at("Ib"), bcol(c)), const(1)], stop=False)
-            unturn("pB", 0, t, "I8", False)
-            group(x0, [const(0)], start=False)
+            group(x0, [(at("Ib"), bcol(c)), const("key")], stop=False)
+            unturn("pB", 0, t, "I8n", True)
             tt(x0, at("ok"), x0, A.max)
-            act(at("x0%d" % t), x0, AF.Identity, bias=127.5)
+            act(at("x0%d" % t), x0, AF.Identity, bias=127.5 - 2.0 ** -17)
         u = [r for r in range(t) if r % 4 == c ^ 1]
-        cut = [(at("B9"), bcol(c)), (at("MG"), at("ones"))] + ([(at("B9n"), bcol(c ^ 1)), (at("B9"), xs_of(u[-1]))] if u else [])
-        group(at("pJ", K, 2 * K), cut, stop=False)
+        cut = [(at("Blk"), bcol(c))] + ([(at("Bneg"), bcol(c ^ 1)), (at("Blk"), xs_of(u[-1]))] if u else [])
         group(at("pW", 0, K), cut + [(at("Ib"), at("NP", t, t + K))], stop=False)
+        if t in XV:
+            big = [(at("B9"), bcol(c)), (at("MG"), at("ones"))] + ([(at("B9n"), bcol(c ^ 1)), (at("B9"), xs_of(u[-1]))] if u else [])
+            group(at("pH", K, 2 * K), big, stop=False)
+        else:
+            group(at("pH", K, 2 * K), [(at("Ib"), bcol(c)), const("less")], stop=False)
         for j, (a, b) in enumerate(PARTS):
             fm, x1, w = of("Fm", t, a, b), of("x1", t, a, b), of("w", t, a, b)
-            tt(fm, at("SCN", 8 * a + 7, 8 * b, 8), at("pB", a, b), A.min)
+            for lo, hi, r in ends("SCN", t, False):
+                tt(of("Fm", t, lo, hi), r, at("pB", lo, hi), A.min)
             ts(x1, fm, MAGIC, 127.0 - MAGIC, A.add, A.add)
-            mm(at("pJ", K + a, K + b), at("B9n"), x1, False, b == K)
-            mm(at("pW", a, b), at("B9n"), x1, False, b == K)
-            tt(at("mx", a, b), x1, at("pJ", K + a, K + b), A.max)
-            tt(xs_of(t, a, b), at("mx", a, b), bcol(c, a, b), A.min)
+            if t in XV:
+                mm(at("pH", K + a, K + b), at("B9n"), x1, False, b == K)
+            mm(at("pW", a, b), at("Bneg"), x1, False, b == K)
+            act(w, at("pW", a, b), AF.Sigmoid, bias=at("mgb"), scale=256.0, accum=at("acc", len(PARTS) * t + j, len(PARTS) * t + j + 1))
+            if t in XV:
+                tt(at("mx", a, b), x1, at("pH", K + a, K + b), A.max)
+                tt(xs_of(t, a, b), at("mx", a, b), bcol(c, a, b), A.min)
+            else:
+                mm(at("pH", K + a, K + b), at("B8"), w, False, b == K)
+                tt(xs_of(t, a, b), x1, at("pH", K + a, K + b), A.max)
             tell(t, a, b)
-            act(at("sg", a, b), at("pW", a, b), AF.Sign)
-            act(w, at("sg", a, b), AF.Relu, accum=at("acc", len(PARTS) * t + j, len(PARTS) * t + j + 1))
         tt(at("q"), at("pT", K, 2 * K), of("w", t), A.mult)
         po = at("P16", 16 * c, 16 * c + 16)
         emit("V", lambda po=po: g.vector.tensor_tensor(out=T.Lf[:].indirect(po[0]), in0=T.q[:], in1=T.Tf[:], op=A.add),
              [at("Lf")], [at("q"), at("Tf"), po], 60 + K * SCATTER)
         if t < RO - 1:
-            group(at("pW", K, 2 * K), [column(o), (at("Ib"), xs_of(t))])
-            act(at("Z", o, o + K), at("pW", K, 2 * K))
-            n = told(t)
-            group(at("pJ", 0, K), [column(n)])
-            for a, b in PARTS:
-                tt(at("Z", n + a, n + b), land_of(t, a, b), at("pJ", a, b), A.add)
+            zput(o, xs_of(t), at("pW", K, 2 * K))
+            if t in ZV:
+                n = told(t)
+                group(at("pB", K, 2 * K), [const("column"), const("told%d" % t)])
+                tt(at("Z", n, n + K), land_of(t), at("pB", K, 2 * K), A.add)
+            else:
+                zput(told(t), land_of(t), at("pW", K, 2 * K))
         for r in {0: [0], 1: [1], 2: [2], 4: [4, 3], 5: [5]}.get(t, ()):
             if r < 4:
                 far_start(r)
                 for a in range(0, K, PIECE):
-                    far_gather(r, a, a + PIECE)
-                far_sums(r, 0, K, True)
-            sources(r)
+                    pieces[len(calls)] = (r, a, a + PIECE)
+                    far_gather(r, a, a + PIECE, line="far")
+                far_max(r, 0, 128)
+                far_max(r, 128, K)
+            else:
+                sources(r)
     dma(T.yl[:], at("Lf"), 4 * NS)
-    dma(T.yx[:, K:2 * K], at("xs5"), 2 * K)
+    dma(T.yx[:, K:2 * K], at("xs5"), 2 * K, q="S")
     n = told(RO - 1)
-    dma(T.yx[:, n:n + K], at("land5"), 2 * K)
-    for start, i in in_order(calls):
-        now[:] = start, start + calls[i][4]
-        calls[i][1]()
+    dma(T.yx[:, n:n + K], at("land5"), 2 * K, q="S")
+    order = in_order(calls)
+    scalar = [i for _, i in order if calls[i][0] == "S"]
+    for i, j in reversed(list(zip(scalar, scalar[1:]))):
+        if i in pieces and j in pieces and pieces[i][0] == pieces[j][0] and pieces[i][2] == pieces[j][1]:
+            pieces[i] = pieces[i][:2] + pieces[j][2:]
+            far_gather(*pieces[i])
+            calls[i], calls[j] = calls.pop(), None
+    for start, i in order:
+        if calls[i]:
+            calls[i][1]()
     for s, n in count.items():
         if n and clk["Y"].get(s, 0) < n:
             g.sync.wait_ge(T.sem[s], n)

from concourse.mybir import AluOpType as A, ActivationFunctionType as AF
import comms_topo

K, W, V, NS, RO = 256, 4096, 1024, 896, 6
MAGIC = 12582912.0
EARLY = (("v", 0, 40), ("k", 40, 112), ("k", 112, 192), ("K", 0, 40), ("K", 40, 112), ("K", 112, 192), ("a", 192, 256), ("H", 0, 0))
PARTS = ((0, 256),)
PIECE = 16
LATE = (("F", 0, 16), ("f", 16, 128), ("f", 128, 256), ("p", 0, 0), ("v", 0, 64), ("v", 64, 128), ("K", 0, 64), ("K", 64, 128), ("M", 0, 128),
        ("M", 128, 256), ("k", 128, 192), ("k", 192, 256), ("n", 0, 0), ("K", 128, 192), ("K", 192, 256), ("H", 0, 0))
GATHER, SCATTER, PE, WAKE, DMA, HOP = 1.56, 3.8, 0.5, 300, 1000, 2800
BF, HF, F3, I3, U1 = "bfloat16", "float16", "float32", "int32", "uint16"
CONST = {"column": (2.0 ** -16, 2.0 ** -17, 1.0, -127.5), "key": (0, 2.0 ** -17, 0, -127.5), "less": (0, -256.0, 0, 0), "rest": (0, -493568.0, 0, 0),
         "flag": (0, 16384.0, 127.0 * 65536 * 128, -0.5)}
CONST.update({"own%d" % _c: (1.0, 256.0 * (_c + 16), 0, 0) for _c in range(4)})
CONST.update({"over%d" % _c: (-1.0, 256.0 * (48 - _c), 127.0 * 65536 * 128, -0.5) for _c in range(4)})
YP = (0, 1, 2, 3)
TH = ()
ZV = (0, 1, 2, 3, 4)
ROOM = 1.0
GATE = 1
SV = (2, 3, 4, 5)
XV = (1, 2, 3)
CONST.update({"told%d" % _t: (0, (14 + 4 * (1 + _t % 3) + _t % 4) / 256, 0, 0) for _t in range(RO - 1)})
SCALED = (("Im", "Ib", -1.0), ("I8n", "Ib", -256.0), ("I13n", "Ib", -8192.0), ("I49", "Ib", 49152.0), ("I49n", "Ib", -49152.0),
          ("I16n", "Ib", -65536.0), ("If", "Ib", 1.0), ("I16f", "Ib", 65536.0), ("Bneg", "Blk", -1.0),
          ("B2", "Blk", 2.0), ("B8", "Blk", 256.0), ("B12", "Blk", 4096.0), ("B53n", "Blk", -53248.0), ("I13", "Ib", 8192.0), ("B9", "Blk", 512.0), ("B9n", "Blk", -512.0), ("B53", "Blk", 53248.0), ("Bf", "Blk", 1.0),
          ("R0n", "R0", -1.0), ("B12f", "Blk", 4096.0))
BANKS = ("pB", "pW", "pD", "pK", "pT", "pH", "pJ", "pO")
_B = {"gr": (64, I3), "pa": (64, I3), "P16": (64, U1), "Q16": (64, U1), "fav": (NS, I3), "Lf": (NS, F3),
      "Si": (V, I3), "S16": (V, U1), "T16": (K, U1), "ysf": (V, F3), "D0": (V, BF), "D1": (V, BF), "RI": (272, BF), "NP": (272, BF),
      "CM": (128 * len(CONST), BF), "acc": (RO * len(PARTS), F3)}
for _d, _w, _l in ((BF, W, "X0 X1 X2 X3 X4 X5 F0 F1 F2 F3 M0 M1 M2"), (F3, W, "Z"), (F3, W // 2, "YV"), (F3, 3 * V, "YS SCN"), (I3, K, "hi z"),
                   (I3, 3 * K, "s2"), (F3, 3 * K, "s1"), (F3, K, "Tf mLQ q ok"), (F3, K * RO, "Fm"), (HF, K, "Th"),
                   (BF, K, "x04 x05 bT xs5 land5"), (BF, 2 * K, "JR"), (BF, K * RO, "x1 w nl"),
                   (I3, 1, "thc mg8 as0 as1 a31 ki ki2 thi tlo mgi mhi mlo"), (F3, 1, "mgf mgb kcf ck nhi lim lim0 k0 k1 ma mb mc"),
                   (BF, 128, "Ib ta tb Blk R0 Dhi MG " + " ".join(_n for _n, _, _ in SCALED if _n[-1] != "f")), (BF, 128 * RO, "Dlo"),
                   (BF, K, "ones mx y0b"), (F3, K, "y0a"), (BF, 144, "WA WB"), (F3, 128, "R8 R8a onf " + " ".join(_n for _n, _, _ in SCALED if _n[-1] == "f"))):
    for _n in _l.split():
        _B[_n] = (_w, _d)
SCRATCH = {n: ("sbuf", [128, w], d) for n, (w, d) in _B.items()}
for _n in BANKS:
    _B[_n] = (1024, BF) if _n == "pO" else (512, F3)
    SCRATCH[_n] = ("psum", [128, _B[_n][0]], _B[_n][1])
SEMAPHORES = ["eV", "eS", "eP", "eG"] + ["d%d" % i for i in range(60)] + [n + "%d_%d" % (t, a) for n in ("arr", "loc") for t in range(RO) for a, _ in PARTS]


def in_order(calls):
    seen, after, row = {}, [], {}
    for i, (q, _, outs, ins, _, _, line) in enumerate(calls):
        dep = set()
        for wr, regs in ((False, ins), (True, outs)):
            for r in regs:
                for j, a, b, w in seen.get(r[1], ()):
                    if (wr or w) and (r[2] < b and a < r[3] or calls[j][0] == q == "P" and r[1] in BANKS):
                        dep.add(j)
        for wr, regs in ((True, outs), (False, ins)):
            for r in regs:
                keep = [e for e in seen.get(r[1], ()) if not (wr and r[2] <= e[1] and e[2] <= r[3] and (q == "P" or r[1] not in BANKS))]
                seen[r[1]] = keep + [(i, r[2], r[3], wr)]
        after.append({j: calls[j][4] + calls[j][5] + (0 if calls[j][0] == q == "P" else WAKE) for j in dep - {i}})
        if line in row:
            after[i].setdefault(row[line], calls[row[line]][4])
        if line:
            row[line] = i
    way = [c[4] + c[5] for c in calls]
    for i in reversed(range(len(calls))):
        for j in after[i]:
            way[j] = max(way[j], after[i][j] + way[i])
    start, busy = {}, {}
    for i in sorted(range(len(calls)), key=lambda i: (-way[i], i)):
        q, _, outs, ins, cost, more, _ = calls[i]
        need = [(q, cost)] + [(b, cost) for b in sorted({r[1] for r in outs + ins if r[1] in BANKS})] + ([("dma", more - DMA)] if more else [])
        t = max([start[j] + after[i][j] for j in after[i]], default=0)
        moved = True
        while moved:
            moved = False
            for res, d in need:
                for a, b, by in busy.get(res, ()):
                    gap = WAKE if res in BANKS and by != q else 0
                    if a < t + d + gap and t < b + gap:
                        t, moved = b + gap, True
        start[i] = t
        for res, d in need:
            busy[res] = sorted(busy.get(res, []) + [(t, t + d, q)])
    return sorted((t, i) for i, t in start.items())


def rank_program(g, core, T, topo):
    rank = T.rank_of(core)
    if rank is None:
        return
    N = len(T.cores)
    queue = {"V": g.vector, "S": g.scalar, "P": g.tensor, "G": g, "Y": g.sync}
    count = {"eV": 0, "eS": 0, "eP": 0, "eG": 0}
    clk = {q: {} for q in queue}
    hist, pieces = {}, {}
    calls = []

    def at(name, c0=0, c1=None, step=1, r0=0, r1=128):
        c1 = _B[name][0] if c1 is None else c1
        ap = T[name][r0:r1, c0:c1] if step == 1 else T[name][r0:r1, c0:c1:step]
        return (ap, name, c0, c1, -(-(c1 - c0) // step), range(r0 // 32, (r1 + 31) // 32))

    def rows(regs):
        return [(r[0], r[1] + str(k)) + r[2:] for r in regs if r[1] in ("JR", "CM") for k in r[5]] + [r for r in regs if r[1] not in ("JR", "CM")]

    def waits(q, me, ins, outs):
        cand = {}
        for wr, regs in ((False, ins), (True, outs)):
            for (_, name, lo, hi, _, _) in regs:
                for rlo, rhi, rw, rme, rsem, rn, rclk in hist.get(name, ()):
                    if rme == me and me == "P":
                        continue
                    if not (lo < rhi and rlo < hi and (wr or rw)) and (rme == me or name not in BANKS):
                        continue
                    if clk[q].get(rsem, 0) < rn and (rsem not in cand or cand[rsem][0] < rn):
                        cand[rsem] = (rn, rclk)
        for s in list(cand):
            n = cand[s][0]
            if not any(o != s and cand[o][1].get(s, 0) >= n for o in cand):
                queue[q].wait_ge(T.sem[s], n)
        for s, (n, rc) in cand.items():
            for a, b in list(rc.items()) + [(s, n)]:
                clk[q][a] = max(clk[q].get(a, 0), b)

    def note(q, me, sem, n, ins, outs):
        count[sem] = n
        snap = dict(clk[q]) if q else {}
        snap[sem] = n
        for w, regs in ((True, outs), (False, ins)):
            for (_, name, lo, hi, _, _) in regs:
                keep = [r for r in hist.get(name, ()) if not (lo <= r[0] and r[1] <= hi and (w or (r[3] == me and not r[2])))]
                hist[name] = keep + [(lo, hi, w, me, sem, n, snap)]

    def emit(q, f, outs, ins, cost, line=None):
        outs, ins = rows(outs), rows(ins)

        def issue():
            waits(q, q, ins, outs)
            f().then_inc(T.sem["e" + q], 1)
            note(q, q, "e" + q, count["e" + q] + 1, ins, outs)
        calls.append((q, issue, outs, ins, max(32 if q == "P" else 64, cost), 0, line))

    def dma(out, in_, size, line=None, q="Y"):
        outs = [out] if isinstance(out, tuple) else []
        ins = [in_] if isinstance(in_, tuple) else []
        s = "d%d" % sum(c[0] != "G" and c[5] > 0 for c in calls)

        def issue():
            waits(q, s, ins, outs)
            queue[q].dma_start(out[0] if outs else out, in_[0] if ins else in_).then_inc(T.sem[s], 16)
            note(q, s, s, 16, ins, outs)
        calls.append((q, issue, outs, ins, 64, DMA + 300 + size // 3, line))

    def half(*regs):
        return 0.5 if all(_B[r[1]][1] in (BF, HF, U1) for r in regs) else 1

    def tt(out, a, b, op, line=None):
        rate = half(out, a, b) * (1 if a[1] in BANKS or b[1] in BANKS else 2)
        emit("V", lambda: g.vector.tensor_tensor(out=out[0], in0=a[0], in1=b[0], op=op), [out], [a, b], out[4] * rate, line)

    def ts(out, a, s1, s2, op0, op1=None, line=None):
        ins = [a] + [s for s in (s1, s2) if isinstance(s, tuple)]
        v1 = s1[0] if isinstance(s1, tuple) else s1
        v2 = s2[0] if isinstance(s2, tuple) else s2
        kw = {} if op1 is None else {"op1": op1}
        emit("V", lambda: g.vector.tensor_scalar(out=out[0], in0=a[0], scalar1=v1, scalar2=v2, op0=op0, **kw), [out], ins, out[4] * half(out, a), line)

    def cp(out, a, line=None):
        emit("V", lambda: g.vector.tensor_copy(out=out[0], in_=a[0]), [out], [a], out[4] * half(out, a), line)

    def ms(out, c):
        emit("V", lambda: g.vector.memset(out[0], c), [out], [], out[4] * half(out))

    def act(out, a, func=AF.Copy, bias=0.0, scale=1.0, accum=None, off=None, line=None):
        ins = [a] + [s for s in (bias, scale, off) if isinstance(s, tuple)]
        kw = {} if accum is None else {"accum_out": accum[0]}
        b, sc = (s[0] if isinstance(s, tuple) else s for s in (bias, scale))
        src = a[0].indirect(off[0]) if off else a[0]
        emit("S", lambda: g.scalar.activation(out=out[0], in_=src, func=func, bias=b, scale=sc, **kw), [out] + ([accum] if accum else []), ins,
             80 + out[4] * GATHER if off else out[4], line)

    def mm(out, l, r, start, stop, gate=(), line=None):
        emit("P", lambda: g.tensor.matmul(out=out[0], lhsT=l[0], rhs=r[0], start=start, stop=stop), [out], [l, r, *gate], PE * max(64, r[4]) * (1 if half(r) < 1 else 4) * (ROOM if out[1] in ("pD", "pK") else 1), line)

    def group(out, pairs, stop=True, gate=(), line=None):
        for i, (l, r) in enumerate(pairs):
            mm(out, l, r, i == 0, stop and i == len(pairs) - 1, gate, line)

    def turn(out, a, line=None):
        emit("P", lambda: g.tensor.transpose(out[0], a[0], T.Ib[:]), [out], [a, at("Ib")], 128 * PE, line)

    def vgather(out, win, off, b=None, op=None, line=None):
        if b is None:
            emit("V", lambda: g.vector.tensor_copy(out=out[0], in_=win[0].indirect(off[0])), [out], [win, off], 60 + out[4] * GATHER, line)
        else:
            emit("V", lambda: g.vector.tensor_tensor(out=out[0], in0=win[0].indirect(off[0]), in1=b[0], op=op), [out], [win, off, b], 60 + out[4] * GATHER, line)

    def iota(out, pattern, base, cm=0, **kw):
        emit("G", lambda: g.iota(out[0], pattern, base, cm, **kw), [out], [], 160 + 2 * out[4])

    def select(out, a, pattern, op, base, cm):
        emit("G", lambda: g.affine_select(out[0], a[0], pattern, op, 0.0, base, cm), [out], [a], 200 + 2 * out[4])

    def tell(t, a, b):
        d = 1 + t % (N - 1)
        nxt, prv = T.cores[(rank + d) % N], T.cores[(rank - d) % N]
        arr, loc, xs, land = "arr%d_%d" % (t, a), "loc%d_%d" % (t, a), xs_of(t, a, b), land_of(t, a, b)

        def issue():
            waits("G", loc, [xs], [])
            rid, pid, _ = topo.addr(nxt)
            g.remote_dma(out_ap=land[0], in_ap=xs[0], remote_sem=T.sem[arr], local_sem=T.sem[loc],
                         pid=pid, routing_id=rid, dma_engine_mask=topo.mask(core, nxt))
            note("G", loc, loc, len(topo.engines(core, nxt)), [xs], [])
            note(None, arr, arr, len(topo.engines(prv, core)), [], [land])
        calls.append(("G", issue, [land], [xs], 600, HOP - 4 * (K - b + a), None))

    def cls(t):
        return t % 4, t % 4 * K

    def paired(t):
        return min([a for what, a, _ in (EARLY if t < 4 else LATE) if what == "a"] + [K])

    def told(t):
        return (1 + t % (N - 1)) * V + t % 4 * K

    def of(name, t, a=0, b=K):
        return at(name, t * K + a, t * K + b)

    def bcol(c, a=0, b=K):
        return at("X0", c * K + a, c * K + b)

    def xs_of(t, a=0, b=K):
        return at("X%d" % (t + 1), t % 4 * K + a, t % 4 * K + b) if t < RO - 1 else at("xs5", a, b)

    def land_of(t, a=0, b=K):
        return at("X%d" % (t + 1), told(t) + a, told(t) + b) if t < RO - 1 else at("land5", a, b)

    def const(name, n=K):
        i, used = list(CONST).index(name), [32 * r for r, v in enumerate(CONST[name]) if v]
        r = dict(r0=used[0], r1=used[0] + 1) if len(used) == 1 else {}
        return (at("CM", 128 * i, 128 * i + 128, **r), at("JR", 0, n, **r))

    def carry(t):
        o, n = t % 4 * K, told(t)
        for lo, hi in ((0, o), (o + K, n), (n + K, W)):
            if lo < hi:
                dma(at("X%d" % (t + 1), lo, hi) if t < RO - 1 else T.yx[:, lo:hi], at("X%d" % t, lo, hi), 2 * (hi - lo), "loads")

    loads = [(at("gr"), T.grant[:]), (at("fav"), T.favor[:])] + [(at("X0", V * i, V * i + V), T.base[:, V * i:V * i + V]) for i in range(N)]
    loads += [(at("Si", 0, K), T.src[:, 0:K]), (at("pa"), T.part[:]), (at("mg8", r1=8), T.mg[:]), (at("thc"), T.th[:]), (at("Si", K, V), T.src[:, K:V])]
    for to, hbm in loads:
        dma(to, hbm, int(to[4] * 4 * half(to)), "loads")

    small = dict(allow_small_or_imprecise_dtypes=True)
    ms(at("ones"), 1.0)
    ms(at("onf"), 1.0)
    ms(at("JR"), 0.0)
    iota(at("JR", 0, K, r1=1), [[1, K]], 0, **small)
    act(at("JR", K, 2 * K, r1=1), at("JR", 0, K, r1=1))
    for r, v, a in ((32, 1.0, 0), (64, 2.0 ** -7, 0), (96, 1.0, 0), (64, 3 * 2.0 ** -8, K)):
        ms(at("JR", a, r0=r, r1=r + 1), v)
    for i, row in enumerate(CONST.values()):
        one = sum(v != 0 for v in row) == 1
        for r, v in enumerate(row):
            if v if one else (r == 0 or v != row[0]):
                to = at("CM", 128 * i, 128 * i + 128, r0=32 * r, r1=32 * r + 1 if r or one else 128)
                ms(to, v) if i < 2 else act(to, at("ones", 0, 128, r0=32 * r, r1=32 * r + 1 if r or one else 128), scale=float(v))
    select(at("R0"), at("ones", 0, 128), [[-16, 8], [0, 16]], A.is_equal, 0, 1)
    select(at("Ib"), at("ones", 0, 128), [[-1, 128]], A.is_equal, 0, 1)
    select(at("WA"), at("ones", 0, 144), [[-16, 9], [1000, 2], [2, 8]], A.is_equal, -1014, 1)
    select(at("WB"), at("ones", 0, 144), [[-16, 9], [1000, 2], [2, 8]], A.is_equal, -1015, 1)
    iota(at("ta"), [[-16, 8], [0, 16]], 0, 1, **small)
    act(at("tb"), at("ta"), AF.Abs, bias=-7.5)
    act(at("Blk"), at("tb"), AF.Sigmoid, scale=-256.0, bias=2048.0)
    select(at("R8a", r1=8), at("onf", r1=8), [[1, 128]], A.is_ge, 0, -16)
    select(at("R8", r1=8), at("R8a", r1=8), [[-1, 128]], A.is_ge, 15, 16)
    iota(at("ki"), [[0, 1]], 0, 1)
    iota(at("RI"), [[0, 17], [1, 16]], 0, **small)
    ms(at("D0"), 2.0 / 16)
    ms(at("D0", 0, V, 8), 512.0)
    ms(at("D1"), -1.0 / 16)
    ms(at("D1", 0, V, 16), 512.0)
    ms(at("as0"), 0)
    for n, m, v in SCALED:
        act(at(n), at(m), scale=v)
    ts(at("ki2"), at("ki"), 15, None, A.bitwise_and)
    cp(at("kcf"), at("ki2"))
    ts(at("ck"), at("kcf"), -4096.0, 128.0 * 65536, A.mult, A.add)
    ts(at("NP"), at("RI"), at("kcf"), -16384.0, A.not_equal, A.mult)
    ts(at("thi"), at("thc"), 4032, None, A.bitwise_and)
    ts(at("tlo"), at("thc"), 63, None, A.bitwise_and)
    ts(at("nhi"), at("thi"), -1.0, None, A.mult)
    ts(at("lim0"), at("tlo"), -1.0, -0.5, A.mult, A.add)
    act(at("Dhi"), at("Ib"), AF.Identity, scale=at("nhi"))
    act(at("Dlo", 0, 128), at("Ib"), AF.Identity, scale=at("lim0"))
    cp(at("mgf", r1=8), at("mg8", r1=8))
    cp(at("P16"), at("gr"))
    cp(at("Lf"), at("fav"))
    cp(at("Q16"), at("pa"))
    for c in range(4):
        cp(at("S16", c * K, c * K + K), at("Si", c * K, c * K + K), None if c else "V")

    def zput(n, x, p, q="S"):
        z, bias = at("Z", n, n + x[4]), (W + n - 512) / 65536
        group(p, [const("column", x[4]), (at("Ib"), x)])
        act(z, p, AF.Identity, bias=bias) if q == "S" else ts(z, p, bias, None, A.add)
    for b in range(8):
        zput(512 * b, at("X0", 512 * b, 512 * b + 512), at(("pB", "pW", "pD", "pH", "pJ", "pK")[b % 6]), "SV"[b % 2])
    mm(at("pK", 0, 1), at("R8", r1=8), at("mgf", r1=8), True, True)
    ts(at("mgb"), at("pK", 0, 1), -256.0, -128.0, A.mult, A.add)
    cp(at("mgi"), at("pK", 0, 1))
    ts(at("mhi"), at("mgi"), 4032, None, A.bitwise_and)
    ts(at("mlo"), at("mgi"), 63, None, A.bitwise_and)
    ts(at("k0"), at("kcf"), 0.0, -512.0, A.is_equal, A.mult)
    ts(at("k1"), at("kcf"), 1.0, -512.0, A.is_equal, A.mult)
    ts(at("ma"), at("mhi"), at("k0"), None, A.mult)
    ts(at("mb"), at("mlo"), 0.5, at("k1"), A.add, A.mult)
    ts(at("mc"), at("ma"), at("mb"), None, A.add)
    act(at("MG"), at("Blk"), AF.Identity, scale=at("mc"))

    def lists(t):
        c = t % 4
        act(at("Tf"), at("Lf"), off=at("P16", 16 * c, 16 * c + 16))
        po = at("P16", 16 * c, 16 * c + 16)
        if t in TH:
            ts(at("Th"), at("Tf"), -2048.0, None, A.add)
        else:
            emit("V", lambda: g.vector.tensor_scalar(out=T.Th[:], in0=T.Lf[:].indirect(po[0]), scalar1=-2048.0, scalar2=None, op0=A.add),
                 [at("Th")], [at("Lf"), po], 60 + K * GATHER)
        n = paired(t)
        for w, h in (("WA", 0), ("WB", n // 2)):
            group(at("pT", h, h + n // 2), [(at(w, 8, 136), at("Th", 0, n, 2)), (at(w, 0, 128), at("Th", 1, n, 2))])
        ts(at("T16", 0, n), at("pT", 0, n), 2048.0, None, A.add)
        if n < K:
            ts(at("T16", n, K), at("Th", n, K), 2048.0, None, A.add)

    def limits(t):
        a, b, n = "as%d" % ((t - 1) % 2), "as%d" % (t % 2), len(PARTS)
        group(at("pH", 0, 1), [(at("Bf"), at("acc", j, j + 1)) for j in range(n * t - n, n * t)])
        tt(at(b), at(a), at("pH", 0, 1), A.add)
        ts(at("a31"), at(b), 31, None, A.bitwise_and)
        ts(at("lim"), at("a31"), -1.0, at("lim0"), A.mult, A.add)
        act(at("Dlo", 128 * t, 128 * t + 128), at("Ib"), AF.Identity, scale=at("lim"))

    def own(t, a=0, b=K):
        return at("X%d" % (0 if t < 4 else t), t % 4 * K + a, t % 4 * K + b)

    def far_start(t):
        for h in (0, 128):
            turn(at("pO", 512 + h, 640 + h), own(t, h, h + 128))
        act(at("bT"), at("pO", 512, 768))
        for h in (0, 128):
            turn(at("pO", h, h + 128), at("bT", h, h + 128), "P" if t >= 4 else None)

    def unturn(p, h, t, scale, stop):
        for a in (0, 128):
            mm(at(p, h + a, h + a + 128), of("nl", t, a, a + 128), at(scale), False, stop and a == 128)

    def far_gather(t, a, b, q="S", line=None):
        out, win, off = at("F%d" % (t % 4), 16 * a, 16 * b), at("X%d" % t), at("S16", t % 4 * K + a, t % 4 * K + b)
        act(out, win, off=off, line=line) if q == "S" else vgather(out, win, off, line=line)

    def far_max(t, a, b, line=None):
        for p in range(16):
            lo = 16 * a + (b - a) * p
            tt(at("M%d" % (t % 3), lo, lo + b - a), at("F%d" % (t % 4), 16 * a + p, 16 * b, 16), at("pO", a, b), A.max, line)

    def far_sums(t, a, b, gate=()):
        f, m, d = "F%d" % (t % 4), "M%d" % (t % 3), "pD" if t < 4 else "pJ"
        for h in range(a, b, 128):
            group(at(d, h, h + 128), [(own(t, h, h + 128), at("Bneg")), (at("ones", 0, 128), at("Dhi"))], stop=False, gate=gate, line="P" if t < 4 else None)
            for p in range(16):
                mm(at(d, h + p, h + 128, 16), at(f, 16 * h + p, 16 * h + 2048, 16), at("Bneg", 0, 128, 16), False, False)
            for p in range(16):
                mm(at(d, h + p, h + 128, 16), at(m, 16 * h + 128 * p, 16 * h + 128 * p + 128), at("B2", 0, 128, 16), False, False)
            mm(at(d, h, h + 128), at("ones", 0, 128), at("Dlo", 128 * t, 128 * t + 128), False, True)

    def far_end(t, line=None):
        act(of("nl", t), at("pD" if t < 4 else "pJ", 0, K), AF.Sigmoid, scale=-256.0, line=line)

    def sources(t):
        c, o = cls(t)
        x0 = bcol(c) if t < 4 else at("x0%d" % t)
        w, blk = of("w", t), at("Si", o, o + K)
        fm, x1, xs = of("Fm", t), of("x1", t), xs_of(t)
        both = t in SV
        favour = [(at("I16f"), fm), const("flag" if both else "over%d" % c), (at("I16n"), x1), (at("I49"), x0), (at("I49n"), xs)]
        p, s1, s2 = {3: "pD", 5: "pJ"}.get(t, "pK"), of("s1", t % 3), of("s2", t % 3)
        group(at(p, 0, K), favour + ([] if both else [(at("B53n"), w)]), stop=both, line="P" if t < 3 else None)
        if not both:
            unturn(p, 0, t, "I13", True)
            act(s1, at(p, 0, K), AF.Relu)
        group(at(p, K, 2 * K), [const("own%d" % c), (at("B53"), w)], stop=False)
        unturn(p, K, t, "I13n", both)
        if both:
            tt(s1, blk, at(p, K, 2 * K), A.max)
            tt(s2, s1, at(p, 0, K), A.max)
        else:
            mm(at(p, K, 2 * K), at("If"), s1, False, True)
            tt(s2, blk, at(p, K, 2 * K), A.max)
        ts(blk, s2, 4095, None, A.bitwise_and)
        cp(at("S16" if t < 2 else "ysf", o, o + K), blk)
        if t >= 2:
            dma(T.ys[:, o:o + K], at("ysf", o, o + K), 4 * K)

    def keys_s(a, b, vector):
        ys, off = at("YS", 8 * a, 8 * b), at("T16", a // 2, b // 2)
        if vector:
            emit("V", lambda: g.vector.tensor_scalar(out=ys[0], in0=T.Z[:].indirect(off[0]), scalar1=-1.0 / 16, scalar2=None, op0=A.add),
                 [ys], [at("Z"), off], 60 + ys[4] * GATHER, "V")
        else:
            act(ys, at("Z"), AF.Identity, bias=-1.0 / 16, off=off, line="S")

    def scan(out, steps, y, line):
        emit("V", lambda: g.vector.tensor_tensor_scan(out=out[0], data0=steps[0], data1=y[0], initial=512.0, op0=A.add, op1=A.min), [out], [steps, y], out[4], line)

    def keys_v(t, a, b):
        n = paired(t)
        vgather(at("YV", 8 * a, 8 * b), at("Z"), at("T16", (n + a) // 2, (n + b) // 2), at("YS", 8 * a, 8 * b), A.min, "V")
        scan(at("SCN", 8 * a, 8 * b), at("D0", 0, 8 * (b - a)), at("YV", 8 * a, 8 * b), "scans")

    def keys_all(t, a, b):
        lo, hi = 16 * a - 8 * paired(t), 16 * b - 8 * paired(t)
        act(at("YS", lo, hi), at("Z"), AF.Identity, bias=14.0 / 16, off=at("T16", a, b), line="S")
        scan(at("SCN", lo, hi), at("D1", 0, hi - lo), at("YS", lo, hi), "scans")

    def ends(name, t, first):
        n = paired(t)
        return [(0, n, at(name, 7, 8 * n, 8))] + ([(n, K, at(name, 8 * n + (0 if first else 15), 16 * K - 8 * n, 16))] if n < K else [])

    def entry(t):
        c = t % 4
        if t in YP:
            mm(at("pH", 0, K), at("R0n"), at("Th"), True, False)
            for a, b, y in ends("YS", t, True):
                mm(at("pH", a, b), at("B12f"), y, False, b == K, line="P")
        else:
            for a, b, y in ends("YS", t, True):
                act(at("y0a", a, b), y, AF.Identity, bias=MAGIC, line="S")
            act(at("y0b"), at("y0a"), AF.Identity, bias=-MAGIC, line="S")
            mm(at("pH", 0, K), at("B12"), at("y0b"), True, True, line="P")
        for a, b, y in ends("YS", t, True) if t in YP else [(0, K, 0)]:
            ts(at("hi", a, b), at("pH", a, b), at("ck"), 65536 * (0 if t not in YP else 0.5 if a == 0 else 0.5 - 15.0 / 16), A.add, A.add, line="V")
        ts(at("z"), at("hi"), 61440, None, A.bitwise_and, line="V")
        vgather(at("mLQ"), at("Lf"), at("Q16", 16 * c, 16 * c + 16), at("z"), A.max, "V")
        group(at("pT", K, 2 * K), [(at("Im"), at("Th")), const("rest"), (at("Bf"), at("mLQ"))])

    for t in range(RO):
        c, o = cls(t)
        carry(t)
        lists(t)
        if t:
            limits(t)
        x0 = at("pB", 0, K)
        if t >= 4:
            far_start(t)
        if t >= 2:
            far_sums(t - 2, 0, K, [at("T16")] if GATE else [])

        plan = EARLY if t < 4 else LATE
        for i, (what, a, b) in enumerate(plan):
            if what in "kv":
                keys_s(a, b, what == "v")
            elif what == "K":
                keys_v(t, a, b)
            elif what == "a":
                keys_all(t, a, b)
            elif what in "fF":
                far_gather(t, a, b, *(("S", "S") if what == "f" else ("V", "V")))
            elif what == "M":
                far_max(t, a, b, "V")
                far_sums(t, a, b)
            elif what == "n":
                far_end(t, "S")
            elif what == "p":
                far_end(t - 2, "S")
            else:
                entry(t)
        if t >= 2:
            if ("p", 0, 0) not in plan:
                far_end(t - 2, "S")
            sources(t - 2)
        if t < 4:
            group(x0, [(at("Ib"), bcol(c)), const("key")])
        else:
            act(at("ok"), xs_of(t - 4), AF.Identity, bias=2.0 ** -17 - 127.5)
            group(x0, [(at("Ib"), bcol(c)), const("key")], stop=False)
            unturn("pB", 0, t, "I8n", True)
            tt(x0, at("ok"), x0, A.max)
            act(at("x0%d" % t), x0, AF.Identity, bias=127.5 - 2.0 ** -17)
        u = [r for r in range(t) if r % 4 == c ^ 1]
        cut = [(at("Blk"), bcol(c))] + ([(at("Bneg"), bcol(c ^ 1)), (at("Blk"), xs_of(u[-1]))] if u else [])
        group(at("pW", 0, K), cut + [(at("Ib"), at("NP", t, t + K))], stop=False)
        if t in XV:
            big = [(at("B9"), bcol(c)), (at("MG"), at("ones"))] + ([(at("B9n"), bcol(c ^ 1)), (at("B9"), xs_of(u[-1]))] if u else [])
            group(at("pH", K, 2 * K), big, stop=False)
        else:
            group(at("pH", K, 2 * K), [(at("Ib"), bcol(c)), const("less")], stop=False)
        for j, (a, b) in enumerate(PARTS):
            fm, x1, w = of("Fm", t, a, b), of("x1", t, a, b), of("w", t, a, b)
            for lo, hi, r in ends("SCN", t, False):
                tt(of("Fm", t, lo, hi), r, at("pB", lo, hi), A.min)
            ts(x1, fm, MAGIC, 127.0 - MAGIC, A.add, A.add)
            if t in XV:
                mm(at("pH", K + a, K + b), at("B9n"), x1, False, b == K)
            mm(at("pW", a, b), at("Bneg"), x1, False, b == K)
            act(w, at("pW", a, b), AF.Sigmoid, bias=at("mgb"), scale=256.0, accum=at("acc", len(PARTS) * t + j, len(PARTS) * t + j + 1))
            if t in XV:
                tt(at("mx", a, b), x1, at("pH", K + a, K + b), A.max)
                tt(xs_of(t, a, b), at("mx", a, b), bcol(c, a, b), A.min)
            else:
                mm(at("pH", K + a, K + b), at("B8"), w, False, b == K)
                tt(xs_of(t, a, b), x1, at("pH", K + a, K + b), A.max)
            tell(t, a, b)
        tt(at("q"), at("pT", K, 2 * K), of("w", t), A.mult)
        po = at("P16", 16 * c, 16 * c + 16)
        emit("V", lambda po=po: g.vector.tensor_tensor(out=T.Lf[:].indirect(po[0]), in0=T.q[:], in1=T.Tf[:], op=A.add),
             [at("Lf")], [at("q"), at("Tf"), po], 60 + K * SCATTER)
        if t < RO - 1:
            zput(o, xs_of(t), at("pW", K, 2 * K))
            if t in ZV:
                n = told(t)
                group(at("pB", K, 2 * K), [const("column"), const("told%d" % t)])
                tt(at("Z", n, n + K), land_of(t), at("pB", K, 2 * K), A.add)
            else:
                zput(told(t), land_of(t), at("pW", K, 2 * K))
        for r in {0: [0], 1: [1], 2: [2], 4: [4, 3], 5: [5]}.get(t, ()):
            if r < 4:
                far_start(r)
                for a in range(0, K, PIECE):
                    pieces[len(calls)] = (r, a, a + PIECE)
                    far_gather(r, a, a + PIECE, line="far")
                far_max(r, 0, 128)
                far_max(r, 128, K)
            else:
                sources(r)
    dma(T.yl[:], at("Lf"), 4 * NS)
    dma(T.yx[:, K:2 * K], at("xs5"), 2 * K, q="S")
    n = told(RO - 1)
    dma(T.yx[:, n:n + K], at("land5"), 2 * K, q="S")
    order = in_order(calls)
    scalar = [i for _, i in order if calls[i][0] == "S"]
    for i, j in reversed(list(zip(scalar, scalar[1:]))):
        if i in pieces and j in pieces and pieces[i][0] == pieces[j][0] and pieces[i][2] == pieces[j][1]:
            pieces[i] = pieces[i][:2] + pieces[j][2:]
            far_gather(*pieces[i])
            calls[i], calls[j] = calls.pop(), None
    for start, i in order:
        if calls[i]:
            calls[i][1]()
    for s, n in count.items():
        if n and clk["Y"].get(s, 0) < n:
            g.sync.wait_ge(T.sem[s], n)
